import numpy as np, ml_dtypes
CORES = [5,29,101,125,133,157,229,253]
N = 8
import mx_ref
BF = ml_dtypes.bfloat16
def gentries(a):
    return np.ascontiguousarray(a.reshape(8, 16, -1).transpose(0, 2, 1)).reshape(8, -1)
def gtable(e):
    e = np.asarray(e); return np.ascontiguousarray(e.reshape(8, -1, 16).transpose(0, 2, 1)).reshape(128, -1).astype(np.int32)
def gcols(t, e):
    v = np.concatenate([t.reshape(8, 16, -1, 4), np.zeros((8, 16, 1, 4), BF)], axis=2)
    return np.ascontiguousarray(np.stack([v[g][:, e[g]] for g in range(8)])).reshape(128, -1)
def tile(rs):
    return np.stack(rs, axis=2).reshape(128, -1).astype(BF)
def cut(t, i, w=512):
    return t[:, w * i:w * i + w]
def pick(q, e):
    c = np.concatenate([q[0].reshape(128, -1, 4), np.zeros((128, 1, 4), np.uint8)], axis=1); s = np.concatenate([q[1], np.ones((16, 1), np.uint8)], axis=1)
    return (np.ascontiguousarray(c[:, e].reshape(128, -1)), np.ascontiguousarray(s[:, e]))
def join(*qs):
    return (np.concatenate([q[0] for q in qs], axis=1), np.concatenate([q[1] for q in qs], axis=1))
def put(q, e, v):
    c, s = q[0].reshape(128, -1, 4).copy(), q[1].copy(); c[:, e] = v[0].reshape(128, -1, 4); s[:, e] = v[1]
    return (c.reshape(128, -1), s)
def pk(c, s):
    return (np.ascontiguousarray(c), mx_ref.live(s))
def emit(q):
    return q[0], q[1]
def packed(v, rng):
    q = [mx_ref.quantize(np.ascontiguousarray(v[r])) for r in range(N)]
    return np.stack([a for a, b in q]), np.stack([mx_ref.plane(b, rng) for a, b in q])
def values_of_codes():
    e, c = np.zeros((128, 128, 4), np.float32), np.zeros((128, 2, 4), np.uint8)
    e[np.arange(128), np.arange(128), 0] = 1
    c[:127, :, 0] = np.arange(256).reshape(2, 128).T[:127]
    return mx_ref.matmul(mx_ref.quantize(e.reshape(128, 512).astype(BF)), (c.reshape(128, 8), np.full((16, 2), 127, np.uint8))).T.reshape(-1).astype(np.float64)
CODE_VALUE, SCALE_VALUE = values_of_codes(), 2.0 ** (np.arange(256) - 127.0)
def decode(q):
    return (CODE_VALUE[q[0]].reshape(16, 8, -1, 4) * SCALE_VALUE[q[1]][:, None, :, None] + 0.0).reshape(128, -1).astype(np.float32)
def f(rng, *shape):
    return mx_ref.flush((rng.standard_normal(shape, dtype=np.float32) * np.exp2(rng.integers(-2, 3, shape[:-1] + (1,)))).astype(BF))
def wide(rng, *shape, cols=0):
    v = rng.standard_normal(shape, dtype=np.float32) * np.exp2(rng.integers(-12, 13, shape)).astype(np.float32)
    if cols: v *= np.repeat(np.exp2(rng.integers(-cols, cols + 1, shape[:-2] + (1, shape[-1] // 4))) * (rng.random(shape[:-2] + (1, shape[-1] // 4)) > 0.0625), 4, axis=-1).astype(np.float32)
    return mx_ref.flush(v.astype(BF))
C, V, K, R = 288, 56, 112, 3
STEP = [1, 2, 4]
def big(v):
    v = v.astype(np.float32)
    v[np.abs(v) < np.float32(2.0 ** -16)] = 0
    return v.astype(BF)
def lists(a):
    return np.stack([gtable(a[r]) for r in range(N)])
def numbers_of(rng):
    return {"x": big(f(rng, N, 128, 4 * C)), "e": big(f(rng, N, 128, 16 * V)), "ex": lists(rng.integers(0, V, (N, 8, 4 * V))), "at": lists(rng.integers(0, V, (N, 8, C))), "u": np.array(f(rng, N, 128, 512)), "v": np.array(f(rng, N, 128, 512))}
def layers(rng):
    return big(f(rng, N, 128, 2048)).reshape(N, 8, 16, 4, 8, 16, 4)
def weights(rng, w):
    c, p = packed(np.ascontiguousarray(w).reshape(N, 128, 2048), rng)
    return {"wc": c, "ws": p}
def signs(rng):
    return np.stack([rng.permutation(8) % 2 * 2.0 - 1.0 for r in range(N)])
def setup_inputs(rng):
    return {**numbers_of(rng), **weights(rng, layers(rng))}
def setup_inputs_ties(rng):
    d = numbers_of(rng)
    o = rng.permutation(N)
    x, e = d["x"].reshape(N, 8, 16, C, 4), d["e"].reshape(N, 8, 16, 4 * V, 4)
    for r in range(N):
        k = np.zeros(C, int) if r == o[0] else rng.permutation(C) % 3
        a = x[r][:, :8, :3].copy()
        a[:, :, 2] = 0
        x[r][:, :8] = a[:, :, k]
        e[r][:, :8] = a[:, :, rng.permutation(4 * V) % 3]
    x[o[1]] = 0
    at = gentries(d["at"][o[1]]).copy()
    for g in rng.permutation(8)[:4]: at[g] = rng.integers(V)
    d["at"][o[1]] = gtable(at)
    u = d["u"].reshape(N, 8, 16, 128, 4)
    u[:, :, 8:, ::16] = 0
    d["x"], d["e"], d["u"] = x.reshape(N, 128, 4 * C), e.reshape(N, 128, 16 * V), u.reshape(N, 128, 512)
    w = layers(rng)
    w[:, :, 8:, :, :, :8] = 0
    return {**d, **weights(rng, w)}
def setup_inputs_near(rng):
    d = numbers_of(rng)
    m = C + 4 * V
    x = np.zeros((N, 8, 16, m, 4), np.float32)
    at = np.zeros((N, 8, C), int)
    u = d["u"].reshape(N, 128, 128, 4)
    u[:, :, ::16] = 0
    o, c = rng.permutation(N) % 4, signs(rng)
    x[:, :, 10:] = rng.integers(4, 8, (N, 8, 6, m, 4)) * 2.0 ** -20
    for r in range(N):
        if o[r] < 2:
            s = ((np.arange(m) + rng.integers(0, C, (8, 1))) % C + 1) // 2
            g = ((s[:, :, None] >> np.arange(8)) & 1) * np.exp2(np.arange(8) - 23.0)
            x[r, :, :2, :, 0] = c[r][:, None, None]
            x[r, :, 8] = g[:, :, :4]
            x[r, :, 9] = g[:, :, 4:]
            at[r] = np.argsort(rng.random((8, V)), axis=1)[:, np.arange(C) // 8]
        else:
            x[r, :, :2, :, 0] = rng.integers(8, 14, (8, 2, m)) * 2.0 ** -31
            at[r] = rng.integers(0, 4, (8, C))
        k = 1.0 if o[r] == 0 else 2.0 ** -30
        for h in range(0, 128, 16):
            u[r, h, h, 0] = k
            u[r, h + 8:h + 10, h] = k
            if o[r] >= 2:
                u[r, h, h, 0] = 9 * 2.0 ** -33
                u[r, h + 1, h, 0] = 8 * 2.0 ** -33
    x = x.astype(BF)
    d["x"], d["e"] = np.ascontiguousarray(x[:, :, :, :C]).reshape(N, 128, 4 * C), np.ascontiguousarray(x[:, :, :, C:]).reshape(N, 128, 16 * V)
    d["at"], d["u"] = lists(at), u.reshape(N, 128, 512)
    w = layers(rng)
    w[:, :, :10] = 0
    w[:, :, :, :, :, :10] = 0
    return {**d, **weights(rng, w)}
def setup_inputs_huge(rng):
    d = numbers_of(rng)
    m = C + 4 * V
    c = rng.integers(0, 2, (N, m)) * 2.0 - 1.0
    c[:, :C] = np.stack([rng.permutation(C) % 2 * 2.0 - 1.0 for r in range(N)])
    c[rng.permutation(N) < N // 2] = -1
    x = ((0.6 + 0.2 * rng.random((N, 128, m, 4))) * np.where(c < 0, -2.0 ** 30, 2.0 ** 28)[:, None, :, None]).astype(np.float32).astype(BF)
    d["x"], d["e"] = np.ascontiguousarray(x[:, :, :C]).reshape(N, 128, 4 * C), np.ascontiguousarray(x[:, :, C:]).reshape(N, 128, 16 * V)
    u = d["u"].reshape(N, 128, 128, 4)
    a = 2.0 ** 30 * (1 - 0.25 * rng.random((N, 128, 8, 4))) * signs(rng)[:, None, :, None]
    u[:, :, ::16] = a.astype(np.float32).astype(BF)
    d["u"] = u.reshape(N, 128, 512)
    w = np.zeros((N, 128, 4, 128, 4), np.float32)
    i = np.arange(128)
    for b in range(4): w[:, i, b, i, b] = 16
    return {**d, **weights(rng, w.astype(BF))}
def setup_inputs_crowd(rng):
    d = setup_inputs(rng)
    at, ex = rng.integers(0, V, (N, 8, C)), rng.integers(0, V, (N, 8, 4 * V))
    for r in range(N):
        for g, i in enumerate(rng.permutation(8)):
            a, b = rng.permutation(V)[:2]
            if i < 4:
                at[r, g] = np.where(rng.permutation(C) < C - i, a, b)
                ex[r, g, 4 * a:4 * a + 4] = a
                ex[r, g, 4 * b:4 * b + 4] = b
            if i == 4: ex[r, g] = a
            if i == 5:
                at[r, g] = rng.integers(K // 4, V, C)
                ex[r, g] = rng.integers(K // 4, V, 4 * V)
            if i == 6:
                at[r, g] = rng.integers(0, K // 4, C)
                ex[r, g] = rng.integers(0, K // 4, 4 * V)
            if i == 7:
                at[r, g] = rng.permutation(C) % V
                ex[r, g] = (np.arange(4 * V) // 4 + 1) % V
    d["ex"], d["at"] = lists(ex), lists(at)
    return d
def setup_inputs_spread(rng):
    d = setup_inputs(rng)
    d["x"], d["e"] = big(wide(rng, N, 128, 4 * C, cols=6)), big(wide(rng, N, 128, 16 * V, cols=6))
    return d
def check_inputs(d):
    b = []
    for k in ("x", "e", "u", "v"):
        a = np.abs(d[k].astype(np.float32))
        if not (np.isfinite(a).all() and ((a == 0) | (a >= 2.0 ** -30) & (a <= 2.0 ** 30)).all()): b.append("a value of " + k)
    for k in ("ex", "at"):
        if ((d[k] < 0) | (d[k] >= V)).any(): b.append("an entry of " + k)
    none, least, most = [emit(mx_ref.quantize(np.full((128, 16), k, np.float32).astype(BF)))[1][0, 0] for k in (0.0, 2.0 ** -30, 2.0 ** 30)]
    for r in range(N):
        if ((d["wc"][r] == 0x7F) | (d["wc"][r] == 0xFF)).any(): b.append("wc: a code that is no number")
        s = mx_ref.live(d["ws"][r])
        if ((s != none) & ((s < least) | (s > most))).any(): b.append("ws: a scale out of range")
    return b
def reference(x, e, ex, at, u, v, wc, ws):
    qu = [mx_ref.quantize(u[r]) for r in range(N)]
    lay = [pk(wc[r], ws[r]) for r in range(N)]
    now, mem = [x[r] for r in range(N)], [e[r] for r in range(N)]
    to, node = [gentries(ex[r]) for r in range(N)], [gentries(at[r]) for r in range(N)]
    rot = [np.zeros((8, V), np.int64) for r in range(N)]
    came_by = [None] * N
    num, group = np.arange(C), np.arange(8)[:, None]
    for t in range(R):
        sent = []
        for r in range(N):
            s = mx_ref.matmul(qu[r], mx_ref.quantize(now[r]))[::16] + np.float32(0.0)
            n, a, b = node[r], s[:, :, None], s[:, None, :]
            first = (n[:, :, None] == n[:, None, :]) & ((a > b) | (a == b) & (num[:, None] < num))
            k = np.sum(first, axis=1)
            way = 4 * n + (rot[r][group, n] + k) % 4
            o = np.lexsort((k, way))
            w = np.take_along_axis(way, o, axis=1)
            follows = np.zeros((8, C), bool)
            follows[:, 1:] = w[:, 1:] == w[:, :-1]
            pred = np.zeros((8, C), np.int64)
            np.put_along_axis(pred, o, np.where(follows, np.roll(o, 1, axis=1), C + w), axis=1)
            last = np.tile(C + np.arange(4 * V), (8, 1))
            g, i = np.nonzero(np.concatenate([~follows[:, 1:], np.ones((8, 1), bool)], axis=1))
            last[g, w[g, i]] = o[g, i]
            p = gcols(np.concatenate([now[r], mem[r]], axis=1), pred)
            z = ((now[r].astype(np.float32) + p.astype(np.float32)) * np.float32(0.5)).astype(BF)
            q = mx_ref.quantize(z)
            h = tile([np.maximum(mx_ref.matmul(pick(lay[r], np.arange(128 * b, 128 * b + 128)), q), np.float32(0.0)) * np.float32(0.03125) + z[:, b::4].astype(np.float32) for b in range(4)])
            mem[r] = gcols(np.concatenate([h, mem[r]], axis=1), last)
            rot[r] = (rot[r] + np.sum(n[:, :, None] == np.arange(V), axis=1)) % 4
            stack = np.lexsort((k, way, to[r][group, way]))
            now[r] = gcols(h, stack)
            came_by[r] = np.take_along_axis(way, stack, axis=1)
            node[r] = to[r][group, came_by[r]]
            sent.append(mx_ref.quantize(np.ascontiguousarray(cut(mem[r], 0, 4 * K))))
        came = decode(join(*sent)).astype(BF)
        for r in range(N): mem[r] = np.concatenate([cut(came, r ^ STEP[t], 4 * K), mem[r][:, 4 * K:]], axis=1)
    y, ot = np.zeros((N, 128, C), np.float32), np.zeros((N, 8, C), np.float32)
    oc, osc = np.zeros((N, 128, 16 * V), np.uint8), np.zeros((N, 16, 4 * V), np.uint8)
    for r in range(N):
        y[r] = mx_ref.matmul(mx_ref.quantize(v[r]), mx_ref.quantize(now[r]))
        ot[r] = came_by[r]
        oc[r], osc[r] = emit(mx_ref.quantize(np.ascontiguousarray(mem[r])))
    return {"y": y, "ot": ot, "oc": oc, "osc": osc}

@@ -1,0 +1,638 @@
+from concourse.mybir import dt, AluOpType, ActivationFunctionType
+
+C, V, K, R = 288, 56, 112, 3
+E = 4 * V
+STEP = [1, 2, 4]
+W0 = 296
+WW = W0 + E
+BIG = 2.0 ** 60
+M4 = 1.5 * 2.0 ** 25
+M17 = 1.5 * 2.0 ** 40
+KB = 144 * 512
+ODD_ON_ACT = [0, 3, 2]
+ACT2 = [10, 14, 12]
+XSPLIT = [10, 18, 18]
+XV = 4
+SRC = [(0, 1), (1, 1), (2, 1)]
+CY, CA, FIX, HOP, GA, SC, DL = 1.0, 1.0, 65, 110, 1.5, 3.5, 1.15
+JIT, TURNS, SEED = 1000, 10, 239
+F, B16, I32, U16, Q8, U8 = "float32", "bfloat16", "int32", "uint16", "float8_e4m3fn_x4", "uint8"
+
+
+def _sb(n, d):
+    return ("sbuf", [128, n], d)
+
+
+SCRATCH = {
+    "ps": ("psum", [128, 4096], F),
+    "lin": _sb(32, I32), "ut": _sb(512, B16), "vt": _sb(512, B16),
+    "wx": _sb(2048, B16), "wh": _sb(2048, B16), "zz": _sb(1152, B16), "xo": _sb(1152, B16),
+    "qu": _sb(128, Q8), "su": _sb(128, U8), "qur": _sb(384, Q8), "sur": _sb(384, U8),
+    "qv": _sb(128, Q8), "sv": _sb(128, U8), "qw": _sb(512, Q8), "sw": _sb(512, U8),
+    "qx": _sb(C, Q8), "sx": _sb(C, U8), "qz": _sb(C, Q8), "sz": _sb(C, U8),
+    "qc": _sb(5 * C, Q8), "sc": _sb(5 * C, U8), "qm": _sb(256, Q8), "sm": _sb(256, U8),
+    "et": _sb(2048, B16), "qe": _sb(512, Q8), "se": _sb(512, U8),
+    "gi": _sb(512, F), "gj": _sb(512, B16), "gt": _sb(512, B16), "qg": _sb(128, Q8), "sg": _sb(128, U8),
+    "hq": _sb(128, Q8), "hs": _sb(128, U8),
+    "ct": _sb(5 * 1152, B16), "st": _sb(C, F), "kr": _sb(C, F), "kd": _sb(C, F), "kc": _sb(18, F),
+    "ja": _sb(4 * C, B16), "cb": _sb(10 * C, B16), "cs": _sb(10 * C, B16), "acc": _sb(18, F),
+    "pa": _sb(18, U16), "pb": _sb(18, U16), "iw": _sb(WW, F), "sg2": _sb(C, F), "pr": _sb(C, F),
+    "opr": _sb(72, U16), "lr": _sb(512, F), "ld": _sb(512, F), "osl": _sb(32, U16), "rb": _sb(1152, F),
+    "yo": _sb(C, F), "oti": _sb(2 * C, I32), "otf": _sb(C, F),
+    "ci": _sb(8, I32), "cf": _sb(16, F), "c2": _sb(512, F), "i16": _sb(32, F), "pk": _sb(24, F), "pku": _sb(24, U16),
+    "xl": _sb(36, F), "xlu": _sb(36, U16), "l2u": _sb(18, U16), "l4u": _sb(14, U16), "lq": _sb(32, U16),
+    "la": _sb(18, U16), "el": _sb(18, F), "cl": _sb(64, F), "du": _sb(28, F), "dms": _sb(80, F),
+    "d16": _sb(512, F), "d4": _sb(C, F), "four": _sb(C, B16), "rm": _sb(4 * C, B16),
+    "lb": _sb(46, B16), "xa": _sb(1024, B16), "xt": _sb(1024, B16), "sk": _sb(512 + 2 * C, F),
+    "a0": _sb(32, F), "ra": _sb(14, F), "xb": _sb(128, F), "xc": _sb(128, F), "rho": _sb(14, U16), "sid": _sb(4, U16),
+    "piw": _sb(E, F), "pid": _sb(E, F), "piu": _sb(14, U16),
+    "qq": _sb(3 * 64, F), "nb": _sb(3 * 112, F), "nt": _sb(128, F), "nd": _sb(E, F), "nl": _sb(56, F),
+    "fa": _sb(4 * 14, F), "tl": _sb(5 * 42, F), "tm": _sb(84, F), "ud": _sb(42, F), "sou": _sb(42, U16), "vou": _sb(42, U16),
+    "fy": _sb(E, F), "fe": _sb(3 * E, F), "fs": _sb(E, F), "pp": _sb(3 * 232, F), "br": _sb(3 * E, F), "bd": _sb(3 * E, F),
+    "pl": _sb(4 * 14, F), "vr": _sb(3 * E, F), "vw": _sb(3 * WW, F), "stw": _sb(3 * WW, F),
+    "vs": _sb(3 * C, F), "vd": _sb(3 * C, F), "vi": _sb(108, I32), "sl": _sb(96, U16), "y1": _sb(C, F),
+}
+for _t in range(R):
+    SCRATCH["qb%d" % _t] = _sb(128, Q8)
+    SCRATCH["sb%d" % _t] = _sb(128, U8)
+    SCRATCH["lc%d" % _t] = _sb(128, Q8)
+    SCRATCH["ls%d" % _t] = _sb(128, U8)
+SEMAPHORES = ["ev", "ea", "ep", "eg", "hop", "hopo", "otd"] + ["d%d" % i for i in range(40)] \
+    + ["arr%d" % t for t in range(R)] + ["out%d" % t for t in range(R)]
+
+A = AluOpType
+AF = ActivationFunctionType
+
+
+def v(name, lo=0, hi=None, step=1):
+    return (name, lo, SCRATCH[name][1][1] if hi is None else hi, step)
+
+
+def width(x):
+    return (x[2] - x[1] + x[3] - 1) // x[3]
+
+
+def two(x):
+    return SCRATCH[x[0]][2] in (B16, U16)
+
+
+def bank(b, n=C):
+    return ("ps", 512 * b, 512 * b + n, 1)
+
+
+_masks = {}
+
+
+def bits(x):
+    if x[0] == "ps":
+        return 1 << (x[1] // 512)
+    k = x[1:]
+    if k not in _masks:
+        m = 0
+        for c in range(x[1], x[2], x[3]):
+            m |= 1 << c
+        _masks[k] = m
+    return _masks[k]
+
+
+def build(T, topo, core, rank):
+    ops = []
+
+    def isind(x):
+        return isinstance(x, tuple) and len(x) == 3
+
+    def ap(x):
+        if isind(x):
+            return ap(x[1]).indirect(ap(x[2]))
+        if isinstance(x, tuple):
+            return T[x[0]][:, x[1]:x[2]] if x[3] == 1 else T[x[0]][:, x[1]:x[2]:x[3]]
+        return x
+
+    def ind(win, off):
+        return ("ind", win, off)
+
+    def op(q, cost, reads, writes, call, **kw):
+        r = []
+        for x in reads:
+            if isinstance(x, tuple):
+                r += [x[1], x[2]] if isind(x) else [x]
+        d = {"q": q, "cost": cost, "r": r, "w": writes, "call": call, "lat": 0.0, "sem": None, "inc": 1}
+        d.update(kw)
+        ops.append(d)
+
+    def vcost(out, src):
+        if isind(src):
+            return FIX + GA * width(out) * CY
+        return FIX + (0.5 if two(out) and two(src) else 1.0) * width(out) * CY
+
+    def copy(out, src):
+        op("v", vcost(out, src), [src], [out], lambda e: e.tensor_copy(ap(out), ap(src)))
+
+    def scatter(win, off, src):
+        op("v", FIX + SC * width(src) * CY, [off, src], [win], lambda e: e.tensor_copy(ap(win).indirect(ap(off)), ap(src)))
+
+    def ts(out, a, s1, o0, s2=None, o1=None):
+        if o1 is None:
+            f = lambda e: e.tensor_scalar(ap(out), ap(a), ap(s1), None, o0)
+        else:
+            f = lambda e: e.tensor_scalar(ap(out), ap(a), ap(s1), ap(s2), o0, o1)
+        op("v", vcost(out, a), [a, s1, s2], [out], f)
+
+    def tt(out, a, b, o):
+        c = vcost(out, a) if isind(a) else FIX + width(out) * CY * (1.0 if a[0] == "ps" else 2.0)
+        op("v", c, [a, b], [out], lambda e: e.tensor_tensor(ap(out), ap(a), ap(b), o))
+
+    def scan(out, a, b, o0, o1):
+        k = 0.5 if two(out) and two(a) and two(b) else 1.0
+        op("v", FIX + k * width(out) * CY, [a, b], [out], lambda e: e.tensor_tensor_scan(ap(out), ap(a), ap(b), 0.0, o0, o1))
+
+    def transp(out, a):
+        op("v", vcost(out, a), [a], [out], lambda e: e.transpose(ap(out), ap(a)))
+
+    def mset(out, val):
+        op("v", vcost(out, out), [], [out], lambda e: e.memset(ap(out), val))
+
+    def quant(q, s, a):
+        op("v", 30 + 0.27 * width(a), [a], [q, s], lambda e: e.quantize_mx(ap(q), ap(s), ap(a)))
+
+    def act(out, a, fn, bias=None, scale=1.0, acc=None):
+        kw = {} if scale == 1.0 else {"scale": scale}
+        if bias is not None:
+            kw["bias"] = ap(bias)
+        if acc is not None:
+            kw["accum_out"] = ap(acc)
+        c = FIX + 15 + width(out) * CA * (GA if isind(a) else 1.0) + (25 if acc else 0)
+        op("a", c, [a, bias], [out] + ([acc] if acc else []), lambda e: e.activation(ap(out), ap(a), fn, **kw))
+
+    def mm(out, lq, ls, rq, rs, start=True, stop=True):
+        op("p", 30 + (width(out) + 16) * 1.1, [lq, ls, rq, rs], [out],
+           lambda e: e.matmul_mx(ap(out), ap(lq), ap(ls), ap(rq), ap(rs), start, stop))
+
+    def iota(out, pat, base=0, cm=0):
+        if SCRATCH[out[0]][2] == I32:
+            f = lambda e: e.iota(ap(out), pat, base, cm)
+        else:
+            f = lambda e: e.iota(ap(out), pat, base, cm, allow_small_or_imprecise_dtypes=True)
+        op("g", 150 + 2 * width(out) * CY, [], [out], f)
+
+    nd = [0]
+
+    def fresh():
+        nd[0] += 1
+        return "d%d" % (nd[0] - 1)
+
+    def dma(q, out, src, reads, writes, nbytes, sem=None):
+        op(q, 100.0, reads, writes, lambda e: e.dma_start(out, src), lat=DL * (1800 + nbytes / 150.0), sem=sem or fresh(), inc=16)
+
+    def add(out, src):
+        op("g", 1000.0, [src, out], [out], lambda e: e.dma_start(ap(out), ap(src), accum_op=A.add), lat=3000.0 * DL,
+           sem=fresh(), inc=16)
+
+    def col(i):
+        return v("cf", i, i + 1)
+
+    def diag16(tmp, row):
+        n = width(row)
+        scan(v(tmp, 0, n), v("d16", 0, n), row, A.mult, A.add)
+        return v(tmp, 15, n, 16)
+
+    dma("s", ap(v("lin", 0, 18)), T.at[:], [], [v("lin", 0, 18)], 9000)
+    dma("a", ap(v("lin", 18, 32)), T.ex[:], [], [v("lin", 18, 32)], 7000)
+    dma("s", ap(v("ut")), T.u[:], [], [v("ut")], 131072)
+    dma("a", ap(v("wx", 0, 576)), T.x[:, 0:576], [], [v("wx", 0, 576)], 280000)
+    dma("s", ap(v("wx", 576, 1152)), T.x[:, 576:1152], [], [v("wx", 576, 1152)], 420000)
+    first = [v("wx", 1151, 1152)]
+    dma("s", ap(v("wx", 1152, 2048)), T.e[:], first, [v("wx", 1152, 2048)], 230000)
+    dma("s", ap(v("qw")).bitcast(dt.uint8), T.wc[:], first, [v("qw")], 500000)
+    dma("s", ap(v("sw")), T.ws[:], first, [v("sw")], 560000)
+    dma("s", ap(v("vt")), T.v[:], first, [v("vt")], 700000)
+
+    iota(v("ci", 0, 1), [[0, 1]], 0, 1)
+    iota(v("i16"), [[16, 32]])
+    iota(v("pk", 0, 8), [[16, 8]])
+    iota(v("pk", 8, 24), [[16, 2], [32, 4], [0, 2]])
+    iota(v("xl"), [[1, 18], [0, 2]])
+    iota(v("c2", 0, C), [[1, C]])
+    iota(v("c2", C, 512), [[2048, V], [513, 4]], KB)
+    iota(v("gi"), [[1, 8], [0, 32], [-1, 2]])
+    iota(v("iw", 0, W0), [[0, W0]])
+    iota(v("iw", W0, WW), [[1, E]], C)
+    for t in range(R):
+        iota(v("stw", t * WW, t * WW + WW), [[0, WW]])
+        iota(v("vw", t * WW, t * WW + WW), [[0, WW]])
+    iota(v("et"), [[0, 2048]], 1)
+    op("g", 170 + 4096 * CY, [v("et")], [v("et")],
+       lambda e: e.affine_select(ap(v("et")), ap(v("et")), [[-1, 4], [1, 512]], A.is_equal, 0.0, 0, -4))
+    p = v("ci", 0, 1)
+    ts(v("ci", 1, 2), p, 15, A.bitwise_and)
+    ts(v("ci", 2, 3), p, 3, A.bitwise_and)
+    ts(v("ci", 3, 4), p, 2, A.logical_shift_right, 3, A.bitwise_and)
+    ts(v("ci", 4, 5), p, 31, A.bitwise_and)
+    ts(v("ci", 5, 6), p, 5, A.logical_shift_right)
+    copy(v("cf", 0, 6), v("ci", 0, 6))
+    cq, ca, cq2, c31 = col(1), col(2), col(3), col(4)
+    f16, f4, f44, acol, h2, kb = col(6), col(7), col(8), col(9), col(10), col(11)
+    ts(f16, cq, 15.0, A.is_equal, 1.0 / BIG, A.max)
+    ts(f4, cq2, 3.0, A.is_equal, 1.0 / BIG, A.max)
+    ts(f44, f4, 4.0, A.mult)
+    ts(acol, ca, -1.0, A.mult, 1.5, A.add)
+    ts(h2, col(5), -2.0, A.mult)
+    ts(kb, ca, float(KB), A.add)
+    copy(v("pku"), v("pk"))
+    copy(v("xlu"), v("xl"))
+    ts(v("l2u"), v("i16", 0, 18), 2.0, A.mult, c31, A.add)
+    ts(v("l4u"), v("i16", 0, 14), 0.25, A.mult, cq2, A.add)
+    ts(v("lq"), v("i16"), 0.0, A.mult, cq, A.add)
+    ts(v("cl", 32, 64), v("i16"), 0.0, A.mult, ca, A.add)
+    ts(v("la"), v("cl", 32, 50), 16.0, A.add)
+    ts(v("el"), v("i16", 0, 18), cq, A.add)
+    ts(v("du", 0, 14), v("el", 0, 14), float(W0), A.add)
+    ts(v("du", 14, 28), v("el", 0, 14), float(W0), A.add)
+    copy(v("fa", 0, 14), v("cl", 32, 46))
+    ts(v("cl", 14, 18), v("el", 0, 4), 0.5, A.add, 2.0 ** 18, A.mult)
+    ts(v("cl", 18, 22), v("el", 0, 4), 2.0 ** 17, A.mult, KB - 0.5, A.add)
+    ts(v("dms", 20, 36), v("c2", 0, 16), cq, A.subtract)
+    ts(v("dms", 36, 40), v("c2", 0, 4), cq2, A.subtract)
+    ts(v("dms", 40, 60), v("dms", 20, 40), 1.0, A.is_equal, BIG, A.mult)
+    ts(v("dms", 60, 80), v("dms", 20, 40), 0.0, A.not_equal)
+    tt(v("dms", 0, 20), v("dms", 40, 60), v("dms", 60, 80), A.max)
+    act(v("d16"), ind(v("dms", 0, 20), v("lq")), AF.Copy)
+    act(v("d4"), ind(v("dms", 0, 20), v("la")), AF.Copy)
+    mset(v("four"), 4.0)
+    mset(v("rm"), 1.0)
+    mset(v("rm", 0, 4 * C, C), 0.0)
+    mset(v("ct", 4 * 1152 + 2, 5 * 1152, 4), 0.0)
+    mset(v("ct", 4 * 1152 + 3, 5 * 1152, 4), 0.0)
+    mset(v("pp", 0, 3 * 232, 232), 0.0)
+    mset(v("pl", 0, 14), 0.0)
+    act(v("gj"), v("gi"), AF.Abs, h2)
+    act(v("gt"), v("gj"), AF.Relu, float(C), -float(C))
+    quant(v("qg"), v("sg"), v("gt"))
+    quant(v("qe"), v("se"), v("et"))
+
+    quant(v("qu"), v("su"), v("ut"))
+    op("v", FIX + 384 * GA * CY, [v("qu"), v("pku")], [v("qur")], lambda e: e.tensor_copy(
+        ap(v("qur")).bitcast(dt.uint32), ap(v("qu")).bitcast(dt.uint32).indirect(ap(v("pku")))))
+    act(v("sur"), ind(v("su"), v("pku")), AF.Copy)
+    quant(v("qv"), v("sv"), v("vt"))
+
+    ts(v("lb", 0, 18), v("lin", 0, 18), 1.0, A.add, 2.0 ** 18, A.mult)
+    ts(v("lb", 32, 46), v("lin", 18, 32), 2.0 ** 17, A.mult)
+    act(v("xa", 576, 1024), ind(v("lb", 32, 46), v("xlu", 0, 28)), AF.Copy)
+    transp(v("xt", 576, 1024), v("xa", 576, 1024))
+    act(v("xa", 0, 576), ind(v("lb", 0, 18), v("xlu")), AF.Copy)
+    transp(v("xt", 0, 576), v("xa", 0, 576))
+    kx = v("sk", C, 512)
+    sk = [v("sk", 0, C), v("sk", 512, 512 + C), v("sk", 512 + C, 512 + 2 * C)]
+    tt(kx, ind(v("xt", 576, 1024), v("l2u", 0, 14)), v("c2", C, 512), A.add)
+    act(sk[0], ind(v("xt", 0, 576), v("l2u")), AF.Copy)
+    nj = [0]
+
+    def junk(n, s=2):
+        nj[0] ^= 1
+        return v("ja", (s + nj[0]) * C, (s + nj[0]) * C + n)
+
+    for m in range(4):
+        act(junk(C), sk[0], AF.Sign, v("cl", 14 + m, 15 + m), -1.0, v("a0", m, m + 1))
+    act(v("xb"), ind(v("a0", 0, 4), v("xlu", 0, 8)), AF.Identity, C / 2.0, 0.5)
+    transp(v("xc"), v("xb"))
+    copy(v("qq", 0, 64), ind(v("xc"), v("l2u", 0, 4)))
+    add(sk[0], v("c2", 0, C))
+    ts(v("tl", 0, 14), v("el", 0, 14), 512.0, A.mult, kb, A.add)
+    tt(v("a0", 18, 32), v("lb", 32, 46), v("tl", 0, 14), A.add)
+    for m in range(14):
+        act(junk(E), kx, AF.Sign, v("a0", 18 + m, 19 + m), -1.0, v("ra", m, m + 1))
+    for m in range(4):
+        act(junk(E), kx, AF.Sign, v("cl", 18 + m, 19 + m), -1.0, v("a0", 8 + m, 9 + m))
+    ts(v("rho"), v("ra"), 0.5, A.mult, (E - 1) / 2.0, A.add)
+    ts(v("sid"), v("a0", 8, 12), 0.5, A.mult, E / 2.0, A.add)
+    scatter(v("piw"), v("rho"), v("c2", 0, E))
+    ts(v("piu"), diag16("pid", v("piw")), f16, A.mult)
+
+    na_ = [0, 112, 168]
+    nd_ = [56, 224, 280]
+
+    def counts(t):
+        q = 64 * t
+        ahi, d = v("nb", na_[t], na_[t] + V), v("nb", nd_[t], nd_[t] + V)
+        tt(ahi, v("qq", q + 1, q + 57), v("qq", q, q + V), A.subtract)
+        if t == 0:
+            copy(d, v("qq", 0, V))
+        else:
+            tt(v("nt", 64, 64 + V), v("qq", q, q + V), v("qq", q - 64, q - 64 + V), A.subtract)
+            tt(d, v("nt", 64, 64 + V), v("nb", na_[t - 1], na_[t - 1] + V), A.subtract)
+        for a in range(4):
+            ts(v("fy", a, E, 4), ahi, 1.5 - a, A.add, M4, A.add)
+        fe, pp = v("fe", E * t, E * t + E), 232 * t
+        act(fe, v("fy"), AF.Identity, -M4)
+        act(v("fs"), ind(fe, v("piu")), AF.Copy)
+        scan(v("pp", pp + 1, pp + E + 1), v("fs"), v("fs"), A.add, A.max)
+        if t < R - 1:
+            act(v("nt", 0, 64), ind(v("pp", pp, pp + E + 1), v("sid")), AF.Copy, scale=0.25)
+            tt(v("qq", q + 64, q + 128), v("nt", 0, 64), v("qq", 0, 64), A.add)
+        act(v("br", E * t, E * t + E), ind(v("pp", pp, pp + E + 1), v("rho")), AF.Copy, scale=0.25)
+        vr = v("vr", E * t, E * t + E)
+        act(vr, ind(d, v("l4u")), AF.Copy)
+        add(vr, kx)
+        if t:
+            add(vr, v("fe", E * t - E, E * t))
+
+    def ends(t, n):
+        w, o = 14 * n, na_[t]
+        scan(v("nd", 0, 8 * w), v("d4", 0, 8 * w), v("nb", o, o + 8 * w), A.mult, A.add)
+        ts(v("nl", 0, 2 * w), v("nd", 3, 8 * w, 4), f4, A.mult)
+        lo, hi, ud = v("fa", 14 * t, 14 * t + w), v("fa", 14 * t + 14, 14 * t + 14 + w), v("ud", 14 * t, 14 * t + w)
+        t0, t1, t2, t3, t4 = [v("tl", 42 * i, 42 * i + w) for i in range(5)]
+        ts(t0, v("nl", 0, w), acol, A.add, M4, A.add)
+        ts(hi, t0, -M4, A.add, ca, A.add)
+        tt(t0, hi, lo, A.is_equal)
+        tt(ud, t0, v("du", 0, w), A.mult)
+        tt(t1, v("nl", w, 2 * w), lo, A.add)
+        tt(t2, v("nl", w, 2 * w), hi, A.add)
+        tt(t3, t1, ud, A.max)
+        tt(t4, t2, ud, A.max)
+        copy(v("sou", 14 * t, 14 * t + w), t3)
+        copy(v("sl", 54 + 14 * t, 54 + 14 * t + w), t4)
+        for i in range(t, t + n):
+            scatter(v("stw", i * WW, i * WW + WW), v("sou", 14 * i, 14 * i + 14), v("iw", W0, WW))
+
+    def sources(t, n):
+        w = 14 * n
+        for i in range(t, t + n):
+            scan(v("bd", E * i, E * i + E), v("d16", 0, E), v("br", E * i, E * i + E), A.mult, A.add)
+        ts(v("pl", 14 * t + 14, 14 * t + 14 + w), v("bd", E * t + 15, E * (t + n), 16), f16, A.mult)
+        t0, t1 = v("tm", 0, w), v("tm", 42, 42 + w)
+        tt(t0, v("pl", 14 * t + 14, 14 * t + 14 + w), v("pl", 14 * t, 14 * t + w), A.subtract)
+        tt(t1, t0, v("ud", 14 * t, 14 * t + w), A.max)
+        copy(v("vou", 14 * t, 14 * t + w), t1)
+        for i in range(t, t + n):
+            vs = v("vs", C * i, C * i + C)
+            scatter(v("vw", i * WW, i * WW + WW), v("vou", 14 * i, 14 * i + 14), v("vr", E * i, E * i + E))
+            scan(vs, v("four"), v("vw", i * WW, i * WW + C), A.add, A.max)
+            scan(v("vd", C * i, C * i + C), v("d16", 0, C), vs, A.mult, A.add)
+            if i < R - 1:
+                act(v("y1"), vs, AF.Identity, M17)
+                act(sk[i + 1], v("y1"), AF.Identity, -2.0 * M17, 2.0)
+                add(sk[i + 1], v("c2", 0, C))
+            else:
+                ts(v("oti", 0, C), vs, float(-KB), A.add)
+                ts(v("oti", C, 2 * C), v("oti", 0, C), 9, A.logical_shift_right, 255, A.bitwise_and)
+                copy(v("otf"), v("oti", C, 2 * C))
+                for gr in range(8):
+                    dma("s", T.ot[gr:gr + 1, :], T["otf"][16 * gr:16 * gr + 1, :], [v("otf")], [], 1200, sem="otd")
+        w = 18 * n
+        ts(v("vi", 0, w), v("vd", C * t + 15, C * (t + n), 16), f16, A.mult)
+        ts(v("vi", 54, 54 + w), v("vi", 0, w), 511, A.bitwise_and)
+        ts(v("sl", 18 * t, 18 * t + w), v("vi", 54, 54 + w), 4.0, A.add)
+
+    counts(0)
+    ends(0, 1)
+    sources(0, 1)
+    counts(1)
+    counts(2)
+    ends(1, 2)
+    for t, n in SRC[1:]:
+        sources(t, n)
+
+    def unpack(t):
+        for b in range(4):
+            mm(bank(b, 128), v("qe", 128 * b, 128 * b + 128), v("se", 128 * b, 128 * b + 128), v("lc%d" % t), v("ls%d" % t))
+        for b in range(4):
+            o = v("wx", 1152 + b, 1152 + 4 * K, 4)
+            if t == R - 1 and b % 2:
+                copy(o, bank(b, K))
+            else:
+                act(o, bank(b, K), AF.Copy)
+
+    def send(t):
+        quant(v("qb%d" % t), v("sb%d" % t), v("wx", 1152, 1152 + 512))
+        mate = T.cores[rank ^ STEP[t]]
+        h = relay(T, topo, core, mate)
+        to, dq, ds, sem = (mate, "lc%d" % t, "ls%d" % t, "arr%d" % t) if h is None else (h, "hq", "hs", "hop")
+        rid, pid = topo.addr(to, core)
+        mask, n = topo.mask(core, to), len(topo.engines(core, to))
+
+        def call(e):
+            e.remote_dma(T[dq][:].bitcast(dt.uint8), T["qb%d" % t][:].bitcast(dt.uint8), T.sem[sem], T.sem["out%d" % t], pid, rid, mask)
+            e.remote_dma(T[ds][:], T["sb%d" % t][:], T.sem[sem], T.sem["out%d" % t], pid, rid, mask)
+        op("g", 300.0, [v("qb%d" % t), v("sb%d" % t)], [], call, sem="out%d" % t, inc=2 * n, lat=1500.0, remote=True)
+        hb = relay(T, topo, mate, core)
+        last = mate if hb is None else hb
+        op("n", 0.0, [v("qb%d" % t), v("sb%d" % t)], [v("lc%d" % t), v("ls%d" % t)], None, sem="arr%d" % t,
+           inc=2 * len(topo.engines(last, core)), lat=DL * (3500.0 if hb is None else 7000.0), remote=True)
+
+    def halve(q, b, lo, hi):
+        o, i = v("wx", 64 * lo + b, 64 * hi, 4), ind(v("wh", 512 * b, 512 * b + 512), v("osl", lo, hi))
+        if q == "v":
+            ts(o, i, 0.5, A.mult)
+        else:
+            act(o, i, AF.Copy, scale=0.5)
+
+    xq, xs = v("qx"), v("sx")
+    for t in range(R):
+        quant(xq, xs, v("wx", 0, 1152))
+        no = ODD_ON_ACT[t]
+        dma("s", ap(v("xo")), ap(v("wx", 0, 1152)), [v("wx", 0, 1152)], [v("xo")], 295000)
+        mm(bank(0), v("qur", 0, 128), v("sur", 0, 128), xq, xs)
+        mm(bank(1), v("qur", 128, 256), v("sur", 128, 256), xq, xs)
+        mm(bank(2), v("qur", 256, 384), v("sur", 256, 384), xq, xs)
+        if no:
+            mm(bank(3), v("qur", 256, 384), v("sur", 256, 384), xq, xs)
+        transp(v("st"), bank(0))
+        for k in range(5):
+            for b in range(2 * k, min(2 * k + 2, 9)):
+                for par in range(2):
+                    o = v("ct", 1152 * k + 2 * (b % 2) + par, 1152 * k + 1152, 4)
+                    s = v("st", 32 * b + 16 * par, 32 * b + 16 * par + 1)
+                    if par == 0 or b >= 9 - no:
+                        act(o, bank(3 if par else 1), AF.Sign, s, -1.0)
+                    else:
+                        ts(o, bank(2), s, A.is_lt)
+            quant(v("qc", C * k, C * k + C), v("sc", C * k, C * k + C), v("ct", 1152 * k, 1152 * k + 1152))
+            mm(bank(4), v("qg"), v("sg"), v("qc", C * k, C * k + C), v("sc", C * k, C * k + C), k == 0, k == 4)
+        tt(v("kr"), bank(4), sk[t], A.add)
+        ts(v("kc"), diag16("kd", v("kr")), f16, A.mult)
+        na = ACT2[t]
+        nv = 18 - na
+        for m in range(na):
+            act(junk(C, 0), v("kr"), AF.Sign, v("kc", m, m + 1), -1.0, v("acc", m, m + 1))
+        for m in range(nv):
+            ts(v("cb", C * m, C * m + C), v("kr"), v("kc", na + m, na + m + 1), A.is_lt, 0.5, A.subtract)
+            if m % 4 == 3 or m == nv - 1:
+                lo = C * (m - m % 4)
+                scan(v("cs", lo, C * m + C), v("rm", 0, C * m + C - lo), v("cb", lo, C * m + C), A.mult, A.add)
+        for name, s in (("pa", 4.0), ("pb", 0.0)):
+            ts(v(name, na, 18), v("cs", C - 1, C * nv, C), C / 2.0 + s, A.add)
+            ts(v(name, 0, na), v("acc", 0, na), 0.5, A.mult, (C - 1) / 2.0 + s, A.add)
+            if name == "pa":
+                scatter(v("iw", 0, W0), v("pa"), v("c2", 0, C))
+        act(v("sg2"), ind(v("stw", t * WW, t * WW + WW), v("pb")), AF.Copy)
+        if t:
+            unpack(t - 1)
+        tt(v("pr"), ind(v("iw", 0, W0), v("pb")), v("sg2"), A.max)
+        scan(v("kd"), v("d4", 0, C), v("pr"), A.mult, A.add)
+        ts(v("opr"), v("kd", 3, C, 4), f44, A.mult, ca, A.add)
+        act(v("lr", 0, C), ind(v("iw", 0, W0), v("sl", 18 * t, 18 * t + 18)), AF.Copy)
+        act(v("lr", C, 512), ind(v("iw"), v("sl", 54 + 14 * t, 68 + 14 * t)), AF.Copy)
+        for b in range(4):
+            act(v("wh", 512 * b + C, 512 * b + 512), v("wx", 1152 + b, 2048, 4), AF.Copy, scale=2.0)
+        tt(v("zz"), ind(v("wx"), v("opr")), v("xo"), A.add)
+        quant(v("qz"), v("sz"), v("zz"))
+        ts(v("osl"), diag16("ld", v("lr")), f16, A.mult)
+        for b in range(4):
+            mm(bank(b), v("qw", 128 * b, 128 * b + 128), v("sw", 128 * b, 128 * b + 128), v("qz"), v("sz"))
+            act(v("rb", C * b, C * b + C), bank(b), AF.Relu, scale=0.03125)
+            tt(v("wh", 512 * b, 512 * b + C), v("rb", C * b, C * b + C), v("zz", b, 1152, 4), A.add)
+        if t == R - 1:
+            for b in range(4):
+                halve("v" if b == 3 else "a", b, 18, 26)
+            send(t)
+            for b in range(4):
+                halve("v" if b >= XV else "a", b, 0, 18)
+            for b in range(4):
+                halve("a", b, 26, 32)
+        else:
+            for b in range(3):
+                halve("a", b, 0, 18)
+            halve("v", 3, 0, XSPLIT[t])
+            if XSPLIT[t] < 18:
+                halve("a", 3, XSPLIT[t], 18)
+            for b in range(4):
+                halve("a", b, 18, 32)
+            send(t)
+    quant(xq, xs, v("wx", 0, 1152))
+    mm(bank(4), v("qv"), v("sv"), xq, xs)
+    copy(v("yo"), bank(4))
+    dma("s", T.y[:], ap(v("yo")), [v("yo")], [], 150000)
+    quant(v("qm", 128, 256), v("sm", 128, 256), v("wx", 1536, 2048))
+    dma("s", T.oc[:, 4 * K:4 * E], ap(v("qm", 144, 256)).bitcast(dt.uint8), [v("qm", 144, 256)], [], 57000)
+    for k in range(4):
+        dma("s", T.osc[4 * k:4 * k + 4, K:E], T["sm"][32 * k:32 * k + 4, 144:256], [v("sm", 144, 256)], [], 500)
+    unpack(R - 1)
+    quant(v("qm", 0, 128), v("sm", 0, 128), v("wx", 1152, 1664))
+    dma("s", T.oc[:, 0:4 * K], ap(v("qm", 0, K)).bitcast(dt.uint8), [v("qm", 0, K)], [], 57000)
+    for k in range(4):
+        dma("a" if k < 3 else "s", T.osc[4 * k:4 * k + 4, 0:K], T["sm"][32 * k:32 * k + 4, 0:K], [v("sm", 0, K)], [], 500)
+    return ops
+
+
+def relay(T, topo, src, dst):
+    if topo.may_write(src, dst):
+        return None
+    can = [c for c in topo.cores_of(src) if T.rank_of(c) is None and topo.may_write(c, dst)]
+    near = [c for c in can if topo.die(c) == topo.die(src)]
+    return (near or can)[0]
+
+
+def plan(ops):
+    live = {}
+    for i, o in enumerate(ops):
+        dep = set()
+        for xs, wr in ((o["r"], False), (o["w"], True)):
+            for x in xs:
+                m, keep = bits(x), []
+                for (j, mj, wj) in live.get(x[0], []):
+                    if j != i and mj & m and (wr or wj or (x[0] == "ps" and ops[j]["q"] != o["q"])):
+                        dep.add(j)
+                    if wr and j != i:
+                        mj &= ~m
+                    if mj:
+                        keep.append((j, mj, wj))
+                keep.append((i, m, wr))
+                live[x[0]] = keep
+        o["dep"] = dep
+    n = len(ops)
+    before = [sorted(o["dep"]) for o in ops]
+    after = [[] for _ in range(n)]
+    for i in range(n):
+        for j in before[i]:
+            after[j].append(i)
+    cost, lat, qs = [o["cost"] for o in ops], [o["lat"] for o in ops], [o["q"] for o in ops]
+
+    def run(rank, pre, post, back):
+        left = [len(x) for x in pre]
+        ready = [lat[i] if back else 0.0 for i in range(n)]
+        start = [0.0] * n
+        busy = {q: [] for q in "vapgsn"}
+        pool = [i for i in range(n) if not left[i]]
+        while pool:
+            i = max(pool, key=lambda k: (rank[k], -k))
+            pool.remove(i)
+            t, line, at = ready[i], busy[qs[i]], 0
+            for at, (a, b) in enumerate(line + [(1e18, 1e18)]):
+                if t + cost[i] <= a:
+                    break
+                t = max(t, b)
+            line.insert(at, (t, t + cost[i]))
+            start[i] = t
+            for k in post[i]:
+                left[k] -= 1
+                gap = 0.0 if qs[i] == "p" and qs[k] == "p" else HOP + lat[k if back else i]
+                ready[k] = max(ready[k], t + cost[i] + gap)
+                if not left[k]:
+                    pool.append(k)
+        return start
+
+    rank = [0.0] * n
+    for i in range(n - 1, -1, -1):
+        rank[i] += cost[i] + lat[i] + HOP
+        for j in before[i]:
+            rank[j] = max(rank[j], rank[i])
+    best, seed = None, SEED
+    for turn in range(TURNS):
+        start = run(rank, before, after, False)
+        end = max(start[i] + cost[i] + lat[i] for i in range(n))
+        if best is None or end <= best[0]:
+            best = (end, start)
+        rank = []
+        for i in range(n):
+            seed = (seed * 1103515245 + 12345) % 2147483648
+            rank.append(best[1][i] + cost[i] + JIT * (seed >> 8) / 8388608.0)
+        late = run(rank, after, before, True)
+        rank = [late[i] + cost[i] for i in range(n)]
+    for i in range(n):
+        ops[i]["start"], ops[i]["end"] = best[1][i], best[0]
+    return sorted(range(n), key=lambda i: (best[1][i], i))
+
+
+def emit(g, T, ops, order):
+    queue = {"v": g.vector, "a": g.scalar, "p": g.tensor, "g": g, "s": g.sync}
+    count, seen = {}, {}
+    for at, i in enumerate(order):
+        o = ops[i]
+        q = o["q"]
+        sem = o["sem"] or "e" + q
+        if q != "n":
+            know = seen.setdefault(q, {})
+            for j in sorted(o["dep"], key=lambda k: -ops[k]["at"]):
+                s, c = ops[j]["mark"]
+                if know.get(s, 0) < c and not (q == "p" and ops[j]["q"] == "p"):
+                    queue[q].wait_ge(T.sem[s], c)
+                    know[s] = c
+                    for s2, c2 in ops[j]["know"].items():
+                        know[s2] = max(know.get(s2, 0), c2)
+            ins = o["call"](queue[q])
+            if not o.get("remote"):
+                ins.then_inc(T.sem[sem], o["inc"])
+        count[sem] = count.get(sem, 0) + o["inc"]
+        o["mark"], o["at"], o["know"] = (sem, count[sem]), at, dict(seen.get(q, {}))
+    for s in sorted(count):
+        g.wait_ge(T.sem[s], count[s])
+
+
+def rank_program(g, core, T, topo):
+    rank = T.rank_of(core)
+    if rank is not None:
+        ops = build(T, topo, core, rank)
+        emit(g, T, ops, plan(ops))
+        return
+    for r, src in enumerate(T.cores):
+        for t in range(R):
+            dst = T.cores[r ^ STEP[t]]
+            if relay(T, topo, src, dst) == core:
+                rid, pid = topo.addr(dst, core)
+                mask = topo.mask(core, dst)
+                g.wait_ge(T.sem.hop, 2 * len(topo.engines(src, core)))
+                g.remote_dma(T["lc%d" % t][:].bitcast(dt.uint8), T.hq[:].bitcast(dt.uint8), T.sem["arr%d" % t], T.sem.hopo, pid, rid, mask)
+                g.remote_dma(T["ls%d" % t][:], T.hs[:], T.sem["arr%d" % t], T.sem.hopo, pid, rid, mask)
+                g.wait_ge(T.sem.hopo, 2 * len(topo.engines(core, dst)))

@@ -9,13 +9,13 @@ BIG = 2.0 ** 60
 M4 = 1.5 * 2.0 ** 25
 M17 = 1.5 * 2.0 ** 40
 KB = 144 * 512
-ODD_ON_ACT = [0, 3, 2]
-ACT2 = [10, 14, 12]
-XSPLIT = [10, 18, 18]
-XV = 4
+ODD_ON_ACT = [0, 2, 2]
+ACT2 = [11, 14, 12]
+XSPLIT = [10, 10, 10]
+XV = 3
 SRC = [(0, 1), (1, 1), (2, 1)]
-CY, CA, FIX, HOP, GA, SC, DL = 1.0, 1.0, 65, 110, 1.5, 3.5, 1.15
-JIT, TURNS, SEED = 1000, 10, 239
+CY, CA, FIX, HOP, GA, SC, DL = 0.95, 0.95, 60, 70, 1.5, 3.5, 1.1
+SPAN, JIT, TURNS, SEED = 4000, 1000, 2500, 1
 F, B16, I32, U16, Q8, U8 = "float32", "bfloat16", "int32", "uint16", "float8_e4m3fn_x4", "uint8"
 
 
@@ -26,7 +26,7 @@ def _sb(n, d):
 SCRATCH = {
     "ps": ("psum", [128, 4096], F),
     "lin": _sb(32, I32), "ut": _sb(512, B16), "vt": _sb(512, B16),
-    "wx": _sb(2048, B16), "wh": _sb(2048, B16), "zz": _sb(1152, B16), "xo": _sb(1152, B16),
+    "wx": _sb(2048, B16), "wh": _sb(2048, B16), "zz": _sb(1664, B16), "xo": _sb(1152, B16),
     "qu": _sb(128, Q8), "su": _sb(128, U8), "qur": _sb(384, Q8), "sur": _sb(384, U8),
     "qv": _sb(128, Q8), "sv": _sb(128, U8), "qw": _sb(512, Q8), "sw": _sb(512, U8),
     "qx": _sb(C, Q8), "sx": _sb(C, U8), "qz": _sb(C, Q8), "sz": _sb(C, U8),
@@ -37,8 +37,8 @@ SCRATCH = {
     "ct": _sb(5 * 1152, B16), "st": _sb(C, F), "kr": _sb(C, F), "kd": _sb(C, F), "kc": _sb(18, F),
     "ja": _sb(4 * C, B16), "cb": _sb(10 * C, B16), "cs": _sb(10 * C, B16), "acc": _sb(18, F),
     "pa": _sb(18, U16), "pb": _sb(18, U16), "iw": _sb(WW, F), "sg2": _sb(C, F), "pr": _sb(C, F),
-    "opr": _sb(72, U16), "lr": _sb(512, F), "ld": _sb(512, F), "osl": _sb(32, U16), "rb": _sb(1152, F),
-    "yo": _sb(C, F), "oti": _sb(2 * C, I32), "otf": _sb(C, F),
+    "opr": _sb(72, U16), "lr": _sb(512, F), "ld": _sb(512, F), "osl": _sb(64, U16), "rb": _sb(4 * 416, F),
+    "yo": _sb(C, F), "oti": _sb(36, I32), "otf": _sb(64, F),
     "ci": _sb(8, I32), "cf": _sb(16, F), "c2": _sb(512, F), "i16": _sb(32, F), "pk": _sb(24, F), "pku": _sb(24, U16),
     "xl": _sb(36, F), "xlu": _sb(36, U16), "l2u": _sb(18, U16), "l4u": _sb(14, U16), "lq": _sb(32, U16),
     "la": _sb(18, U16), "el": _sb(18, F), "cl": _sb(64, F), "du": _sb(28, F), "dms": _sb(80, F),
@@ -80,7 +80,7 @@ def bank(b, n=C):
     return ("ps", 512 * b, 512 * b + n, 1)
 
 
-_masks = {}
+_masks, _plans = {}, {}
 
 
 def bits(x):
@@ -153,7 +153,7 @@ def build(T, topo, core, rank):
         op("v", vcost(out, out), [], [out], lambda e: e.memset(ap(out), val))
 
     def quant(q, s, a):
-        op("v", 30 + 0.27 * width(a), [a], [q, s], lambda e: e.quantize_mx(ap(q), ap(s), ap(a)))
+        op("v", 20 + 0.27 * CY * width(a), [a], [q, s], lambda e: e.quantize_mx(ap(q), ap(s), ap(a)))
 
     def act(out, a, fn, bias=None, scale=1.0, acc=None):
         kw = {} if scale == 1.0 else {"scale": scale}
@@ -258,9 +258,13 @@ def build(T, topo, core, rank):
     tt(v("dms", 0, 20), v("dms", 40, 60), v("dms", 60, 80), A.max)
     act(v("d16"), ind(v("dms", 0, 20), v("lq")), AF.Copy)
     act(v("d4"), ind(v("dms", 0, 20), v("la")), AF.Copy)
-    mset(v("four"), 4.0)
-    mset(v("rm"), 1.0)
-    mset(v("rm", 0, 4 * C, C), 0.0)
+    iota(v("four"), [[0, C]], 4)
+    iota(v("rm"), [[0, 4 * C]], 1)
+    op("g", 170 + 8 * C * CY, [v("rm")], [v("rm")],
+       lambda e: e.affine_select(ap(v("rm")), ap(v("rm")), [[0, 4], [1, C]], A.not_equal, 0.0, 0, 0))
+    mset(v("otf", 18, 32), 0.0)
+    for b in range(4):
+        iota(v("rb", 416 * b + C, 416 * b + 416), [[0, 128]])
     mset(v("ct", 4 * 1152 + 2, 5 * 1152, 4), 0.0)
     mset(v("ct", 4 * 1152 + 3, 5 * 1152, 4), 0.0)
     mset(v("pp", 0, 3 * 232, 232), 0.0)
@@ -375,11 +379,13 @@ def build(T, topo, core, rank):
                 act(sk[i + 1], v("y1"), AF.Identity, -2.0 * M17, 2.0)
                 add(sk[i + 1], v("c2", 0, C))
             else:
-                ts(v("oti", 0, C), vs, float(-KB), A.add)
-                ts(v("oti", C, 2 * C), v("oti", 0, C), 9, A.logical_shift_right, 255, A.bitwise_and)
-                copy(v("otf"), v("oti", C, 2 * C))
+                ts(v("oti", 0, 18), v("vd", C * i + 15, C * i + C, 16), f16, A.mult, 256.0 * 512 - KB, A.add)
+                ts(v("oti", 18, 36), v("oti", 0, 18), 9, A.logical_shift_right, 255, A.bitwise_and)
+                copy(v("otf", 0, 18), v("oti", 18, 36))
+                transp(v("otf", 32, 64), v("otf", 0, 32))
                 for gr in range(8):
-                    dma("s", T.ot[gr:gr + 1, :], T["otf"][16 * gr:16 * gr + 1, :], [v("otf")], [], 1200, sem="otd")
+                    p0, c0 = 32 * (gr // 2), 32 + 16 * (gr % 2)
+                    dma("s", T.ot[gr:gr + 1, :], T["otf"][p0:p0 + 18, c0:c0 + 16], [v("otf", 32, 64)], [], 1200, sem="otd")
         w = 18 * n
         ts(v("vi", 0, w), v("vd", C * t + 15, C * (t + n), 16), f16, A.mult)
         ts(v("vi", 54, 54 + w), v("vi", 0, w), 511, A.bitwise_and)
@@ -474,18 +480,25 @@ def build(T, topo, core, rank):
         ts(v("opr"), v("kd", 3, C, 4), f44, A.mult, ca, A.add)
         act(v("lr", 0, C), ind(v("iw", 0, W0), v("sl", 18 * t, 18 * t + 18)), AF.Copy)
         act(v("lr", C, 512), ind(v("iw"), v("sl", 54 + 14 * t, 68 + 14 * t)), AF.Copy)
+        m0 = 128 if t == R - 1 else 0
         for b in range(4):
-            act(v("wh", 512 * b + C, 512 * b + 512), v("wx", 1152 + b, 2048, 4), AF.Copy, scale=2.0)
-        tt(v("zz"), ind(v("wx"), v("opr")), v("xo"), A.add)
-        quant(v("qz"), v("sz"), v("zz"))
-        ts(v("osl"), diag16("ld", v("lr")), f16, A.mult)
+            act(v("wh", 512 * b + C + m0, 512 * b + 512), v("wx", 1152 + 4 * m0 + b, 2048, 4), AF.Copy, scale=2.0)
+        if t == R - 1:
+            act(v("zz", 1152, 1664), v("wx", 1152, 1664), AF.Copy, scale=2.0)
+            scan(v("pid", 0, 128), v("d4", 0, 128), v("lr", C, C + 128), A.mult, A.add)
+            ts(v("osl", 32, 64), v("pid", 3, 128, 4), f44, A.mult, ca, A.add)
+        tt(v("zz", 0, 1152), ind(v("wx"), v("opr")), v("xo"), A.add)
+        quant(v("qz"), v("sz"), v("zz", 0, 1152))
+        ts(v("osl", 0, 32), diag16("ld", v("lr")), f16, A.mult)
         for b in range(4):
             mm(bank(b), v("qw", 128 * b, 128 * b + 128), v("sw", 128 * b, 128 * b + 128), v("qz"), v("sz"))
-            act(v("rb", C * b, C * b + C), bank(b), AF.Relu, scale=0.03125)
-            tt(v("wh", 512 * b, 512 * b + C), v("rb", C * b, C * b + C), v("zz", b, 1152, 4), A.add)
+            act(v("rb", 416 * b, 416 * b + C), bank(b), AF.Relu, scale=0.03125)
+            tt(v("wh", 512 * b, 512 * b + C), v("rb", 416 * b, 416 * b + C), v("zz", b, 1152, 4), A.add)
         if t == R - 1:
+            act(v("xo", 0, 512), ind(v("zz"), v("osl", 32, 64)), AF.Copy)
             for b in range(4):
-                halve("v" if b == 3 else "a", b, 18, 26)
+                tt(v("xo", 512 + b, 1024, 4), ind(v("rb", 416 * b, 416 * b + 416), v("osl", 18, 26)), v("xo", b, 512, 4), A.add)
+            ts(v("wx", 1152, 1664), v("xo", 512, 1024), 0.5, A.mult)
             send(t)
             for b in range(4):
                 halve("v" if b >= XV else "a", b, 0, 18)
@@ -573,23 +586,31 @@ def plan(ops):
                     pool.append(k)
         return start
 
-    rank = [0.0] * n
-    for i in range(n - 1, -1, -1):
-        rank[i] += cost[i] + lat[i] + HOP
-        for j in before[i]:
-            rank[j] = max(rank[j], rank[i])
-    best, seed = None, SEED
-    for turn in range(TURNS):
-        start = run(rank, before, after, False)
-        end = max(start[i] + cost[i] + lat[i] for i in range(n))
-        if best is None or end <= best[0]:
-            best = (end, start)
-        rank = []
-        for i in range(n):
+    key = (tuple(cost), tuple(lat), tuple(qs), tuple(tuple(x) for x in before))
+    if key not in _plans:
+        rank = [0.0] * n
+        for i in range(n - 1, -1, -1):
+            rank[i] += cost[i] + lat[i] + HOP
+            for j in before[i]:
+                rank[j] = max(rank[j], rank[i])
+        best, seed = None, SEED
+        for turn in range(TURNS):
+            start = run(rank, before, after, False)
+            end = max(start[i] + cost[i] + lat[i] for i in range(n))
+            if best is None or end <= best[0]:
+                best = (end, start)
             seed = (seed * 1103515245 + 12345) % 2147483648
-            rank.append(best[1][i] + cost[i] + JIT * (seed >> 8) / 8388608.0)
-        late = run(rank, after, before, True)
-        rank = [late[i] + cost[i] for i in range(n)]
+            mid, rank = best[0] * (seed >> 8) / 8388608.0, []
+            for i in range(n):
+                seed = (seed * 1103515245 + 12345) % 2147483648
+                rank.append(best[1][i] + (JIT * (seed >> 8) / 8388608.0 if abs(best[1][i] - mid) < SPAN else 0.5 * JIT))
+            if turn % 2:
+                rank = [-x for x in rank]
+            else:
+                late = run([rank[i] + cost[i] for i in range(n)], after, before, True)
+                rank = [late[i] + cost[i] for i in range(n)]
+        _plans[key] = best
+    best = _plans[key]
     for i in range(n):
         ops[i]["start"], ops[i]["end"] = best[1][i], best[0]
     return sorted(range(n), key=lambda i: (best[1][i], i))

from concourse.mybir import dt, AluOpType, ActivationFunctionType

C, V, K, R = 288, 56, 112, 3
E = 4 * V
STEP = [1, 2, 4]
W0 = 296
WW = W0 + E
BIG = 2.0 ** 60
M4 = 1.5 * 2.0 ** 25
M17 = 1.5 * 2.0 ** 40
KB = 144 * 512
ODD_ON_ACT = [0, 2, 2]
ACT2 = [11, 14, 12]
XSPLIT = [10, 10, 10]
XV = 3
SRC = [(0, 1), (1, 1), (2, 1)]
CY, CA, FIX, HOP, GA, SC, DL = 0.95, 0.95, 60, 70, 1.5, 3.5, 1.1
SPAN, JIT, TURNS, SEED = 4000, 1000, 2500, 1
F, B16, I32, U16, Q8, U8 = "float32", "bfloat16", "int32", "uint16", "float8_e4m3fn_x4", "uint8"


def _sb(n, d):
    return ("sbuf", [128, n], d)


SCRATCH = {
    "ps": ("psum", [128, 4096], F),
    "lin": _sb(32, I32), "ut": _sb(512, B16), "vt": _sb(512, B16),
    "wx": _sb(2048, B16), "wh": _sb(2048, B16), "zz": _sb(1664, B16), "xo": _sb(1152, B16),
    "qu": _sb(128, Q8), "su": _sb(128, U8), "qur": _sb(384, Q8), "sur": _sb(384, U8),
    "qv": _sb(128, Q8), "sv": _sb(128, U8), "qw": _sb(512, Q8), "sw": _sb(512, U8),
    "qx": _sb(C, Q8), "sx": _sb(C, U8), "qz": _sb(C, Q8), "sz": _sb(C, U8),
    "qc": _sb(5 * C, Q8), "sc": _sb(5 * C, U8), "qm": _sb(256, Q8), "sm": _sb(256, U8),
    "et": _sb(2048, B16), "qe": _sb(512, Q8), "se": _sb(512, U8),
    "gi": _sb(512, F), "gj": _sb(512, B16), "gt": _sb(512, B16), "qg": _sb(128, Q8), "sg": _sb(128, U8),
    "hq": _sb(128, Q8), "hs": _sb(128, U8),
    "ct": _sb(5 * 1152, B16), "st": _sb(C, F), "kr": _sb(C, F), "kd": _sb(C, F), "kc": _sb(18, F),
    "ja": _sb(4 * C, B16), "cb": _sb(10 * C, B16), "cs": _sb(10 * C, B16), "acc": _sb(18, F),
    "pa": _sb(18, U16), "pb": _sb(18, U16), "iw": _sb(WW, F), "sg2": _sb(C, F), "pr": _sb(C, F),
    "opr": _sb(72, U16), "lr": _sb(512, F), "ld": _sb(512, F), "osl": _sb(64, U16), "rb": _sb(4 * 416, F),
    "yo": _sb(C, F), "oti": _sb(36, I32), "otf": _sb(64, F),
    "ci": _sb(8, I32), "cf": _sb(16, F), "c2": _sb(512, F), "i16": _sb(32, F), "pk": _sb(24, F), "pku": _sb(24, U16),
    "xl": _sb(36, F), "xlu": _sb(36, U16), "l2u": _sb(18, U16), "l4u": _sb(14, U16), "lq": _sb(32, U16),
    "la": _sb(18, U16), "el": _sb(18, F), "cl": _sb(64, F), "du": _sb(28, F), "dms": _sb(80, F),
    "d16": _sb(512, F), "d4": _sb(C, F), "four": _sb(C, B16), "rm": _sb(4 * C, B16),
    "lb": _sb(46, B16), "xa": _sb(1024, B16), "xt": _sb(1024, B16), "sk": _sb(512 + 2 * C, F),
    "a0": _sb(32, F), "ra": _sb(14, F), "xb": _sb(128, F), "xc": _sb(128, F), "rho": _sb(14, U16), "sid": _sb(4, U16),
    "piw": _sb(E, F), "pid": _sb(E, F), "piu": _sb(14, U16),
    "qq": _sb(3 * 64, F), "nb": _sb(3 * 112, F), "nt": _sb(128, F), "nd": _sb(E, F), "nl": _sb(56, F),
    "fa": _sb(4 * 14, F), "tl": _sb(5 * 42, F), "tm": _sb(84, F), "ud": _sb(42, F), "sou": _sb(42, U16), "vou": _sb(42, U16),
    "fy": _sb(E, F), "fe": _sb(3 * E, F), "fs": _sb(E, F), "pp": _sb(3 * 232, F), "br": _sb(3 * E, F), "bd": _sb(3 * E, F),
    "pl": _sb(4 * 14, F), "vr": _sb(3 * E, F), "vw": _sb(3 * WW, F), "stw": _sb(3 * WW, F),
    "vs": _sb(3 * C, F), "vd": _sb(3 * C, F), "vi": _sb(108, I32), "sl": _sb(96, U16), "y1": _sb(C, F),
}
for _t in range(R):
    SCRATCH["qb%d" % _t] = _sb(128, Q8)
    SCRATCH["sb%d" % _t] = _sb(128, U8)
    SCRATCH["lc%d" % _t] = _sb(128, Q8)
    SCRATCH["ls%d" % _t] = _sb(128, U8)
SEMAPHORES = ["ev", "ea", "ep", "eg", "hop", "hopo", "otd"] + ["d%d" % i for i in range(40)] \
    + ["arr%d" % t for t in range(R)] + ["out%d" % t for t in range(R)]

A = AluOpType
AF = ActivationFunctionType


def v(name, lo=0, hi=None, step=1):
    return (name, lo, SCRATCH[name][1][1] if hi is None else hi, step)


def width(x):
    return (x[2] - x[1] + x[3] - 1) // x[3]


def two(x):
    return SCRATCH[x[0]][2] in (B16, U16)


def bank(b, n=C):
    return ("ps", 512 * b, 512 * b + n, 1)


_masks, _plans = {}, {}


def bits(x):
    if x[0] == "ps":
        return 1 << (x[1] // 512)
    k = x[1:]
    if k not in _masks:
        m = 0
        for c in range(x[1], x[2], x[3]):
            m |= 1 << c
        _masks[k] = m
    return _masks[k]


def build(T, topo, core, rank):
    ops = []

    def isind(x):
        return isinstance(x, tuple) and len(x) == 3

    def ap(x):
        if isind(x):
            return ap(x[1]).indirect(ap(x[2]))
        if isinstance(x, tuple):
            return T[x[0]][:, x[1]:x[2]] if x[3] == 1 else T[x[0]][:, x[1]:x[2]:x[3]]
        return x

    def ind(win, off):
        return ("ind", win, off)

    def op(q, cost, reads, writes, call, **kw):
        r = []
        for x in reads:
            if isinstance(x, tuple):
                r += [x[1], x[2]] if isind(x) else [x]
        d = {"q": q, "cost": cost, "r": r, "w": writes, "call": call, "lat": 0.0, "sem": None, "inc": 1}
        d.update(kw)
        ops.append(d)

    def vcost(out, src):
        if isind(src):
            return FIX + GA * width(out) * CY
        return FIX + (0.5 if two(out) and two(src) else 1.0) * width(out) * CY

    def copy(out, src):
        op("v", vcost(out, src), [src], [out], lambda e: e.tensor_copy(ap(out), ap(src)))

    def scatter(win, off, src):
        op("v", FIX + SC * width(src) * CY, [off, src], [win], lambda e: e.tensor_copy(ap(win).indirect(ap(off)), ap(src)))

    def ts(out, a, s1, o0, s2=None, o1=None):
        if o1 is None:
            f = lambda e: e.tensor_scalar(ap(out), ap(a), ap(s1), None, o0)
        else:
            f = lambda e: e.tensor_scalar(ap(out), ap(a), ap(s1), ap(s2), o0, o1)
        op("v", vcost(out, a), [a, s1, s2], [out], f)

    def tt(out, a, b, o):
        c = vcost(out, a) if isind(a) else FIX + width(out) * CY * (1.0 if a[0] == "ps" else 2.0)
        op("v", c, [a, b], [out], lambda e: e.tensor_tensor(ap(out), ap(a), ap(b), o))

    def scan(out, a, b, o0, o1):
        k = 0.5 if two(out) and two(a) and two(b) else 1.0
        op("v", FIX + k * width(out) * CY, [a, b], [out], lambda e: e.tensor_tensor_scan(ap(out), ap(a), ap(b), 0.0, o0, o1))

    def transp(out, a):
        op("v", vcost(out, a), [a], [out], lambda e: e.transpose(ap(out), ap(a)))

    def mset(out, val):
        op("v", vcost(out, out), [], [out], lambda e: e.memset(ap(out), val))

    def quant(q, s, a):
        op("v", 20 + 0.27 * CY * width(a), [a], [q, s], lambda e: e.quantize_mx(ap(q), ap(s), ap(a)))

    def act(out, a, fn, bias=None, scale=1.0, acc=None):
        kw = {} if scale == 1.0 else {"scale": scale}
        if bias is not None:
            kw["bias"] = ap(bias)
        if acc is not None:
            kw["accum_out"] = ap(acc)
        c = FIX + 15 + width(out) * CA * (GA if isind(a) else 1.0) + (25 if acc else 0)
        op("a", c, [a, bias], [out] + ([acc] if acc else []), lambda e: e.activation(ap(out), ap(a), fn, **kw))

    def mm(out, lq, ls, rq, rs, start=True, stop=True):
        op("p", 30 + (width(out) + 16) * 1.1, [lq, ls, rq, rs], [out],
           lambda e: e.matmul_mx(ap(out), ap(lq), ap(ls), ap(rq), ap(rs), start, stop))

    def iota(out, pat, base=0, cm=0):
        if SCRATCH[out[0]][2] == I32:
            f = lambda e: e.iota(ap(out), pat, base, cm)
        else:
            f = lambda e: e.iota(ap(out), pat, base, cm, allow_small_or_imprecise_dtypes=True)
        op("g", 150 + 2 * width(out) * CY, [], [out], f)

    nd = [0]

    def fresh():
        nd[0] += 1
        return "d%d" % (nd[0] - 1)

    def dma(q, out, src, reads, writes, nbytes, sem=None):
        op(q, 100.0, reads, writes, lambda e: e.dma_start(out, src), lat=DL * (1800 + nbytes / 150.0), sem=sem or fresh(), inc=16)

    def add(out, src):
        op("g", 1000.0, [src, out], [out], lambda e: e.dma_start(ap(out), ap(src), accum_op=A.add), lat=3000.0 * DL,
           sem=fresh(), inc=16)

    def col(i):
        return v("cf", i, i + 1)

    def diag16(tmp, row):
        n = width(row)
        scan(v(tmp, 0, n), v("d16", 0, n), row, A.mult, A.add)
        return v(tmp, 15, n, 16)

    dma("s", ap(v("lin", 0, 18)), T.at[:], [], [v("lin", 0, 18)], 9000)
    dma("a", ap(v("lin", 18, 32)), T.ex[:], [], [v("lin", 18, 32)], 7000)
    dma("s", ap(v("ut")), T.u[:], [], [v("ut")], 131072)
    dma("a", ap(v("wx", 0, 576)), T.x[:, 0:576], [], [v("wx", 0, 576)], 280000)
    dma("s", ap(v("wx", 576, 1152)), T.x[:, 576:1152], [], [v("wx", 576, 1152)], 420000)
    first = [v("wx", 1151, 1152)]
    dma("s", ap(v("wx", 1152, 2048)), T.e[:], first, [v("wx", 1152, 2048)], 230000)
    dma("s", ap(v("qw")).bitcast(dt.uint8), T.wc[:], first, [v("qw")], 500000)
    dma("s", ap(v("sw")), T.ws[:], first, [v("sw")], 560000)
    dma("s", ap(v("vt")), T.v[:], first, [v("vt")], 700000)

    iota(v("ci", 0, 1), [[0, 1]], 0, 1)
    iota(v("i16"), [[16, 32]])
    iota(v("pk", 0, 8), [[16, 8]])
    iota(v("pk", 8, 24), [[16, 2], [32, 4], [0, 2]])
    iota(v("xl"), [[1, 18], [0, 2]])
    iota(v("c2", 0, C), [[1, C]])
    iota(v("c2", C, 512), [[2048, V], [513, 4]], KB)
    iota(v("gi"), [[1, 8], [0, 32], [-1, 2]])
    iota(v("iw", 0, W0), [[0, W0]])
    iota(v("iw", W0, WW), [[1, E]], C)
    for t in range(R):
        iota(v("stw", t * WW, t * WW + WW), [[0, WW]])
        iota(v("vw", t * WW, t * WW + WW), [[0, WW]])
    iota(v("et"), [[0, 2048]], 1)
    op("g", 170 + 4096 * CY, [v("et")], [v("et")],
       lambda e: e.affine_select(ap(v("et")), ap(v("et")), [[-1, 4], [1, 512]], A.is_equal, 0.0, 0, -4))
    p = v("ci", 0, 1)
    ts(v("ci", 1, 2), p, 15, A.bitwise_and)
    ts(v("ci", 2, 3), p, 3, A.bitwise_and)
    ts(v("ci", 3, 4), p, 2, A.logical_shift_right, 3, A.bitwise_and)
    ts(v("ci", 4, 5), p, 31, A.bitwise_and)
    ts(v("ci", 5, 6), p, 5, A.logical_shift_right)
    copy(v("cf", 0, 6), v("ci", 0, 6))
    cq, ca, cq2, c31 = col(1), col(2), col(3), col(4)
    f16, f4, f44, acol, h2, kb = col(6), col(7), col(8), col(9), col(10), col(11)
    ts(f16, cq, 15.0, A.is_equal, 1.0 / BIG, A.max)
    ts(f4, cq2, 3.0, A.is_equal, 1.0 / BIG, A.max)
    ts(f44, f4, 4.0, A.mult)
    ts(acol, ca, -1.0, A.mult, 1.5, A.add)
    ts(h2, col(5), -2.0, A.mult)
    ts(kb, ca, float(KB), A.add)
    copy(v("pku"), v("pk"))
    copy(v("xlu"), v("xl"))
    ts(v("l2u"), v("i16", 0, 18), 2.0, A.mult, c31, A.add)
    ts(v("l4u"), v("i16", 0, 14), 0.25, A.mult, cq2, A.add)
    ts(v("lq"), v("i16"), 0.0, A.mult, cq, A.add)
    ts(v("cl", 32, 64), v("i16"), 0.0, A.mult, ca, A.add)
    ts(v("la"), v("cl", 32, 50), 16.0, A.add)
    ts(v("el"), v("i16", 0, 18), cq, A.add)
    ts(v("du", 0, 14), v("el", 0, 14), float(W0), A.add)
    ts(v("du", 14, 28), v("el", 0, 14), float(W0), A.add)
    copy(v("fa", 0, 14), v("cl", 32, 46))
    ts(v("cl", 14, 18), v("el", 0, 4), 0.5, A.add, 2.0 ** 18, A.mult)
    ts(v("cl", 18, 22), v("el", 0, 4), 2.0 ** 17, A.mult, KB - 0.5, A.add)
    ts(v("dms", 20, 36), v("c2", 0, 16), cq, A.subtract)
    ts(v("dms", 36, 40), v("c2", 0, 4), cq2, A.subtract)
    ts(v("dms", 40, 60), v("dms", 20, 40), 1.0, A.is_equal, BIG, A.mult)
    ts(v("dms", 60, 80), v("dms", 20, 40), 0.0, A.not_equal)
    tt(v("dms", 0, 20), v("dms", 40, 60), v("dms", 60, 80), A.max)
    act(v("d16"), ind(v("dms", 0, 20), v("lq")), AF.Copy)
    act(v("d4"), ind(v("dms", 0, 20), v("la")), AF.Copy)
    iota(v("four"), [[0, C]], 4)
    iota(v("rm"), [[0, 4 * C]], 1)
    op("g", 170 + 8 * C * CY, [v("rm")], [v("rm")],
       lambda e: e.affine_select(ap(v("rm")), ap(v("rm")), [[0, 4], [1, C]], A.not_equal, 0.0, 0, 0))
    mset(v("otf", 18, 32), 0.0)
    for b in range(4):
        iota(v("rb", 416 * b + C, 416 * b + 416), [[0, 128]])
    mset(v("ct", 4 * 1152 + 2, 5 * 1152, 4), 0.0)
    mset(v("ct", 4 * 1152 + 3, 5 * 1152, 4), 0.0)
    mset(v("pp", 0, 3 * 232, 232), 0.0)
    mset(v("pl", 0, 14), 0.0)
    act(v("gj"), v("gi"), AF.Abs, h2)
    act(v("gt"), v("gj"), AF.Relu, float(C), -float(C))
    quant(v("qg"), v("sg"), v("gt"))
    quant(v("qe"), v("se"), v("et"))

    quant(v("qu"), v("su"), v("ut"))
    op("v", FIX + 384 * GA * CY, [v("qu"), v("pku")], [v("qur")], lambda e: e.tensor_copy(
        ap(v("qur")).bitcast(dt.uint32), ap(v("qu")).bitcast(dt.uint32).indirect(ap(v("pku")))))
    act(v("sur"), ind(v("su"), v("pku")), AF.Copy)
    quant(v("qv"), v("sv"), v("vt"))

    ts(v("lb", 0, 18), v("lin", 0, 18), 1.0, A.add, 2.0 ** 18, A.mult)
    ts(v("lb", 32, 46), v("lin", 18, 32), 2.0 ** 17, A.mult)
    act(v("xa", 576, 1024), ind(v("lb", 32, 46), v("xlu", 0, 28)), AF.Copy)
    transp(v("xt", 576, 1024), v("xa", 576, 1024))
    act(v("xa", 0, 576), ind(v("lb", 0, 18), v("xlu")), AF.Copy)
    transp(v("xt", 0, 576), v("xa", 0, 576))
    kx = v("sk", C, 512)
    sk = [v("sk", 0, C), v("sk", 512, 512 + C), v("sk", 512 + C, 512 + 2 * C)]
    tt(kx, ind(v("xt", 576, 1024), v("l2u", 0, 14)), v("c2", C, 512), A.add)
    act(sk[0], ind(v("xt", 0, 576), v("l2u")), AF.Copy)
    nj = [0]

    def junk(n, s=2):
        nj[0] ^= 1
        return v("ja", (s + nj[0]) * C, (s + nj[0]) * C + n)

    for m in range(4):
        act(junk(C), sk[0], AF.Sign, v("cl", 14 + m, 15 + m), -1.0, v("a0", m, m + 1))
    act(v("xb"), ind(v("a0", 0, 4), v("xlu", 0, 8)), AF.Identity, C / 2.0, 0.5)
    transp(v("xc"), v("xb"))
    copy(v("qq", 0, 64), ind(v("xc"), v("l2u", 0, 4)))
    add(sk[0], v("c2", 0, C))
    ts(v("tl", 0, 14), v("el", 0, 14), 512.0, A.mult, kb, A.add)
    tt(v("a0", 18, 32), v("lb", 32, 46), v("tl", 0, 14), A.add)
    for m in range(14):
        act(junk(E), kx, AF.Sign, v("a0", 18 + m, 19 + m), -1.0, v("ra", m, m + 1))
    for m in range(4):
        act(junk(E), kx, AF.Sign, v("cl", 18 + m, 19 + m), -1.0, v("a0", 8 + m, 9 + m))
    ts(v("rho"), v("ra"), 0.5, A.mult, (E - 1) / 2.0, A.add)
    ts(v("sid"), v("a0", 8, 12), 0.5, A.mult, E / 2.0, A.add)
    scatter(v("piw"), v("rho"), v("c2", 0, E))
    ts(v("piu"), diag16("pid", v("piw")), f16, A.mult)

    na_ = [0, 112, 168]
    nd_ = [56, 224, 280]

    def counts(t):
        q = 64 * t
        ahi, d = v("nb", na_[t], na_[t] + V), v("nb", nd_[t], nd_[t] + V)
        tt(ahi, v("qq", q + 1, q + 57), v("qq", q, q + V), A.subtract)
        if t == 0:
            copy(d, v("qq", 0, V))
        else:
            tt(v("nt", 64, 64 + V), v("qq", q, q + V), v("qq", q - 64, q - 64 + V), A.subtract)
            tt(d, v("nt", 64, 64 + V), v("nb", na_[t - 1], na_[t - 1] + V), A.subtract)
        for a in range(4):
            ts(v("fy", a, E, 4), ahi, 1.5 - a, A.add, M4, A.add)
        fe, pp = v("fe", E * t, E * t + E), 232 * t
        act(fe, v("fy"), AF.Identity, -M4)
        act(v("fs"), ind(fe, v("piu")), AF.Copy)
        scan(v("pp", pp + 1, pp + E + 1), v("fs"), v("fs"), A.add, A.max)
        if t < R - 1:
            act(v("nt", 0, 64), ind(v("pp", pp, pp + E + 1), v("sid")), AF.Copy, scale=0.25)
            tt(v("qq", q + 64, q + 128), v("nt", 0, 64), v("qq", 0, 64), A.add)
        act(v("br", E * t, E * t + E), ind(v("pp", pp, pp + E + 1), v("rho")), AF.Copy, scale=0.25)
        vr = v("vr", E * t, E * t + E)
        act(vr, ind(d, v("l4u")), AF.Copy)
        add(vr, kx)
        if t:
            add(vr, v("fe", E * t - E, E * t))

    def ends(t, n):
        w, o = 14 * n, na_[t]
        scan(v("nd", 0, 8 * w), v("d4", 0, 8 * w), v("nb", o, o + 8 * w), A.mult, A.add)
        ts(v("nl", 0, 2 * w), v("nd", 3, 8 * w, 4), f4, A.mult)
        lo, hi, ud = v("fa", 14 * t, 14 * t + w), v("fa", 14 * t + 14, 14 * t + 14 + w), v("ud", 14 * t, 14 * t + w)
        t0, t1, t2, t3, t4 = [v("tl", 42 * i, 42 * i + w) for i in range(5)]
        ts(t0, v("nl", 0, w), acol, A.add, M4, A.add)
        ts(hi, t0, -M4, A.add, ca, A.add)
        tt(t0, hi, lo, A.is_equal)
        tt(ud, t0, v("du", 0, w), A.mult)
        tt(t1, v("nl", w, 2 * w), lo, A.add)
        tt(t2, v("nl", w, 2 * w), hi, A.add)
        tt(t3, t1, ud, A.max)
        tt(t4, t2, ud, A.max)
        copy(v("sou", 14 * t, 14 * t + w), t3)
        copy(v("sl", 54 + 14 * t, 54 + 14 * t + w), t4)
        for i in range(t, t + n):
            scatter(v("stw", i * WW, i * WW + WW), v("sou", 14 * i, 14 * i + 14), v("iw", W0, WW))

    def sources(t, n):
        w = 14 * n
        for i in range(t, t + n):
            scan(v("bd", E * i, E * i + E), v("d16", 0, E), v("br", E * i, E * i + E), A.mult, A.add)
        ts(v("pl", 14 * t + 14, 14 * t + 14 + w), v("bd", E * t + 15, E * (t + n), 16), f16, A.mult)
        t0, t1 = v("tm", 0, w), v("tm", 42, 42 + w)
        tt(t0, v("pl", 14 * t + 14, 14 * t + 14 + w), v("pl", 14 * t, 14 * t + w), A.subtract)
        tt(t1, t0, v("ud", 14 * t, 14 * t + w), A.max)
        copy(v("vou", 14 * t, 14 * t + w), t1)
        for i in range(t, t + n):
            vs = v("vs", C * i, C * i + C)
            scatter(v("vw", i * WW, i * WW + WW), v("vou", 14 * i, 14 * i + 14), v("vr", E * i, E * i + E))
            scan(vs, v("four"), v("vw", i * WW, i * WW + C), A.add, A.max)
            scan(v("vd", C * i, C * i + C), v("d16", 0, C), vs, A.mult, A.add)
            if i < R - 1:
                act(v("y1"), vs, AF.Identity, M17)
                act(sk[i + 1], v("y1"), AF.Identity, -2.0 * M17, 2.0)
                add(sk[i + 1], v("c2", 0, C))
            else:
                ts(v("oti", 0, 18), v("vd", C * i + 15, C * i + C, 16), f16, A.mult, 256.0 * 512 - KB, A.add)
                ts(v("oti", 18, 36), v("oti", 0, 18), 9, A.logical_shift_right, 255, A.bitwise_and)
                copy(v("otf", 0, 18), v("oti", 18, 36))
                transp(v("otf", 32, 64), v("otf", 0, 32))
                for gr in range(8):
                    p0, c0 = 32 * (gr // 2), 32 + 16 * (gr % 2)
                    dma("s", T.ot[gr:gr + 1, :], T["otf"][p0:p0 + 18, c0:c0 + 16], [v("otf", 32, 64)], [], 1200, sem="otd")
        w = 18 * n
        ts(v("vi", 0, w), v("vd", C * t + 15, C * (t + n), 16), f16, A.mult)
        ts(v("vi", 54, 54 + w), v("vi", 0, w), 511, A.bitwise_and)
        ts(v("sl", 18 * t, 18 * t + w), v("vi", 54, 54 + w), 4.0, A.add)

    counts(0)
    ends(0, 1)
    sources(0, 1)
    counts(1)
    counts(2)
    ends(1, 2)
    for t, n in SRC[1:]:
        sources(t, n)

    def unpack(t):
        for b in range(4):
            mm(bank(b, 128), v("qe", 128 * b, 128 * b + 128), v("se", 128 * b, 128 * b + 128), v("lc%d" % t), v("ls%d" % t))
        for b in range(4):
            o = v("wx", 1152 + b, 1152 + 4 * K, 4)
            if t == R - 1 and b % 2:
                copy(o, bank(b, K))
            else:
                act(o, bank(b, K), AF.Copy)

    def send(t):
        quant(v("qb%d" % t), v("sb%d" % t), v("wx", 1152, 1152 + 512))
        mate = T.cores[rank ^ STEP[t]]
        h = relay(T, topo, core, mate)
        to, dq, ds, sem = (mate, "lc%d" % t, "ls%d" % t, "arr%d" % t) if h is None else (h, "hq", "hs", "hop")
        rid, pid = topo.addr(to, core)
        mask, n = topo.mask(core, to), len(topo.engines(core, to))

        def call(e):
            e.remote_dma(T[dq][:].bitcast(dt.uint8), T["qb%d" % t][:].bitcast(dt.uint8), T.sem[sem], T.sem["out%d" % t], pid, rid, mask)
            e.remote_dma(T[ds][:], T["sb%d" % t][:], T.sem[sem], T.sem["out%d" % t], pid, rid, mask)
        op("g", 300.0, [v("qb%d" % t), v("sb%d" % t)], [], call, sem="out%d" % t, inc=2 * n, lat=1500.0, remote=True)
        hb = relay(T, topo, mate, core)
        last = mate if hb is None else hb
        op("n", 0.0, [v("qb%d" % t), v("sb%d" % t)], [v("lc%d" % t), v("ls%d" % t)], None, sem="arr%d" % t,
           inc=2 * len(topo.engines(last, core)), lat=DL * (3500.0 if hb is None else 7000.0), remote=True)

    def halve(q, b, lo, hi):
        o, i = v("wx", 64 * lo + b, 64 * hi, 4), ind(v("wh", 512 * b, 512 * b + 512), v("osl", lo, hi))
        if q == "v":
            ts(o, i, 0.5, A.mult)
        else:
            act(o, i, AF.Copy, scale=0.5)

    xq, xs = v("qx"), v("sx")
    for t in range(R):
        quant(xq, xs, v("wx", 0, 1152))
        no = ODD_ON_ACT[t]
        dma("s", ap(v("xo")), ap(v("wx", 0, 1152)), [v("wx", 0, 1152)], [v("xo")], 295000)
        mm(bank(0), v("qur", 0, 128), v("sur", 0, 128), xq, xs)
        mm(bank(1), v("qur", 128, 256), v("sur", 128, 256), xq, xs)
        mm(bank(2), v("qur", 256, 384), v("sur", 256, 384), xq, xs)
        if no:
            mm(bank(3), v("qur", 256, 384), v("sur", 256, 384), xq, xs)
        transp(v("st"), bank(0))
        for k in range(5):
            for b in range(2 * k, min(2 * k + 2, 9)):
                for par in range(2):
                    o = v("ct", 1152 * k + 2 * (b % 2) + par, 1152 * k + 1152, 4)
                    s = v("st", 32 * b + 16 * par, 32 * b + 16 * par + 1)
                    if par == 0 or b >= 9 - no:
                        act(o, bank(3 if par else 1), AF.Sign, s, -1.0)
                    else:
                        ts(o, bank(2), s, A.is_lt)
            quant(v("qc", C * k, C * k + C), v("sc", C * k, C * k + C), v("ct", 1152 * k, 1152 * k + 1152))
            mm(bank(4), v("qg"), v("sg"), v("qc", C * k, C * k + C), v("sc", C * k, C * k + C), k == 0, k == 4)
        tt(v("kr"), bank(4), sk[t], A.add)
        ts(v("kc"), diag16("kd", v("kr")), f16, A.mult)
        na = ACT2[t]
        nv = 18 - na
        for m in range(na):
            act(junk(C, 0), v("kr"), AF.Sign, v("kc", m, m + 1), -1.0, v("acc", m, m + 1))
        for m in range(nv):
            ts(v("cb", C * m, C * m + C), v("kr"), v("kc", na + m, na + m + 1), A.is_lt, 0.5, A.subtract)
            if m % 4 == 3 or m == nv - 1:
                lo = C * (m - m % 4)
                scan(v("cs", lo, C * m + C), v("rm", 0, C * m + C - lo), v("cb", lo, C * m + C), A.mult, A.add)
        for name, s in (("pa", 4.0), ("pb", 0.0)):
            ts(v(name, na, 18), v("cs", C - 1, C * nv, C), C / 2.0 + s, A.add)
            ts(v(name, 0, na), v("acc", 0, na), 0.5, A.mult, (C - 1) / 2.0 + s, A.add)
            if name == "pa":
                scatter(v("iw", 0, W0), v("pa"), v("c2", 0, C))
        act(v("sg2"), ind(v("stw", t * WW, t * WW + WW), v("pb")), AF.Copy)
        if t:
            unpack(t - 1)
        tt(v("pr"), ind(v("iw", 0, W0), v("pb")), v("sg2"), A.max)
        scan(v("kd"), v("d4", 0, C), v("pr"), A.mult, A.add)
        ts(v("opr"), v("kd", 3, C, 4), f44, A.mult, ca, A.add)
        act(v("lr", 0, C), ind(v("iw", 0, W0), v("sl", 18 * t, 18 * t + 18)), AF.Copy)
        act(v("lr", C, 512), ind(v("iw"), v("sl", 54 + 14 * t, 68 + 14 * t)), AF.Copy)
        m0 = 128 if t == R - 1 else 0
        for b in range(4):
            act(v("wh", 512 * b + C + m0, 512 * b + 512), v("wx", 1152 + 4 * m0 + b, 2048, 4), AF.Copy, scale=2.0)
        if t == R - 1:
            act(v("zz", 1152, 1664), v("wx", 1152, 1664), AF.Copy, scale=2.0)
            scan(v("pid", 0, 128), v("d4", 0, 128), v("lr", C, C + 128), A.mult, A.add)
            ts(v("osl", 32, 64), v("pid", 3, 128, 4), f44, A.mult, ca, A.add)
        tt(v("zz", 0, 1152), ind(v("wx"), v("opr")), v("xo"), A.add)
        quant(v("qz"), v("sz"), v("zz", 0, 1152))
        ts(v("osl", 0, 32), diag16("ld", v("lr")), f16, A.mult)
        for b in range(4):
            mm(bank(b), v("qw", 128 * b, 128 * b + 128), v("sw", 128 * b, 128 * b + 128), v("qz"), v("sz"))
            act(v("rb", 416 * b, 416 * b + C), bank(b), AF.Relu, scale=0.03125)
            tt(v("wh", 512 * b, 512 * b + C), v("rb", 416 * b, 416 * b + C), v("zz", b, 1152, 4), A.add)
        if t == R - 1:
            act(v("xo", 0, 512), ind(v("zz"), v("osl", 32, 64)), AF.Copy)
            for b in range(4):
                tt(v("xo", 512 + b, 1024, 4), ind(v("rb", 416 * b, 416 * b + 416), v("osl", 18, 26)), v("xo", b, 512, 4), A.add)
            ts(v("wx", 1152, 1664), v("xo", 512, 1024), 0.5, A.mult)
            send(t)
            for b in range(4):
                halve("v" if b >= XV else "a", b, 0, 18)
            for b in range(4):
                halve("a", b, 26, 32)
        else:
            for b in range(3):
                halve("a", b, 0, 18)
            halve("v", 3, 0, XSPLIT[t])
            if XSPLIT[t] < 18:
                halve("a", 3, XSPLIT[t], 18)
            for b in range(4):
                halve("a", b, 18, 32)
            send(t)
    quant(xq, xs, v("wx", 0, 1152))
    mm(bank(4), v("qv"), v("sv"), xq, xs)
    copy(v("yo"), bank(4))
    dma("s", T.y[:], ap(v("yo")), [v("yo")], [], 150000)
    quant(v("qm", 128, 256), v("sm", 128, 256), v("wx", 1536, 2048))
    dma("s", T.oc[:, 4 * K:4 * E], ap(v("qm", 144, 256)).bitcast(dt.uint8), [v("qm", 144, 256)], [], 57000)
    for k in range(4):
        dma("s", T.osc[4 * k:4 * k + 4, K:E], T["sm"][32 * k:32 * k + 4, 144:256], [v("sm", 144, 256)], [], 500)
    unpack(R - 1)
    quant(v("qm", 0, 128), v("sm", 0, 128), v("wx", 1152, 1664))
    dma("s", T.oc[:, 0:4 * K], ap(v("qm", 0, K)).bitcast(dt.uint8), [v("qm", 0, K)], [], 57000)
    for k in range(4):
        dma("a" if k < 3 else "s", T.osc[4 * k:4 * k + 4, 0:K], T["sm"][32 * k:32 * k + 4, 0:K], [v("sm", 0, K)], [], 500)
    return ops


def relay(T, topo, src, dst):
    if topo.may_write(src, dst):
        return None
    can = [c for c in topo.cores_of(src) if T.rank_of(c) is None and topo.may_write(c, dst)]
    near = [c for c in can if topo.die(c) == topo.die(src)]
    return (near or can)[0]


def plan(ops):
    live = {}
    for i, o in enumerate(ops):
        dep = set()
        for xs, wr in ((o["r"], False), (o["w"], True)):
            for x in xs:
                m, keep = bits(x), []
                for (j, mj, wj) in live.get(x[0], []):
                    if j != i and mj & m and (wr or wj or (x[0] == "ps" and ops[j]["q"] != o["q"])):
                        dep.add(j)
                    if wr and j != i:
                        mj &= ~m
                    if mj:
                        keep.append((j, mj, wj))
                keep.append((i, m, wr))
                live[x[0]] = keep
        o["dep"] = dep
    n = len(ops)
    before = [sorted(o["dep"]) for o in ops]
    after = [[] for _ in range(n)]
    for i in range(n):
        for j in before[i]:
            after[j].append(i)
    cost, lat, qs = [o["cost"] for o in ops], [o["lat"] for o in ops], [o["q"] for o in ops]

    def run(rank, pre, post, back):
        left = [len(x) for x in pre]
        ready = [lat[i] if back else 0.0 for i in range(n)]
        start = [0.0] * n
        busy = {q: [] for q in "vapgsn"}
        pool = [i for i in range(n) if not left[i]]
        while pool:
            i = max(pool, key=lambda k: (rank[k], -k))
            pool.remove(i)
            t, line, at = ready[i], busy[qs[i]], 0
            for at, (a, b) in enumerate(line + [(1e18, 1e18)]):
                if t + cost[i] <= a:
                    break
                t = max(t, b)
            line.insert(at, (t, t + cost[i]))
            start[i] = t
            for k in post[i]:
                left[k] -= 1
                gap = 0.0 if qs[i] == "p" and qs[k] == "p" else HOP + lat[k if back else i]
                ready[k] = max(ready[k], t + cost[i] + gap)
                if not left[k]:
                    pool.append(k)
        return start

    key = (tuple(cost), tuple(lat), tuple(qs), tuple(tuple(x) for x in before))
    if key not in _plans:
        rank = [0.0] * n
        for i in range(n - 1, -1, -1):
            rank[i] += cost[i] + lat[i] + HOP
            for j in before[i]:
                rank[j] = max(rank[j], rank[i])
        best, seed = None, SEED
        for turn in range(TURNS):
            start = run(rank, before, after, False)
            end = max(start[i] + cost[i] + lat[i] for i in range(n))
            if best is None or end <= best[0]:
                best = (end, start)
            seed = (seed * 1103515245 + 12345) % 2147483648
            mid, rank = best[0] * (seed >> 8) / 8388608.0, []
            for i in range(n):
                seed = (seed * 1103515245 + 12345) % 2147483648
                rank.append(best[1][i] + (JIT * (seed >> 8) / 8388608.0 if abs(best[1][i] - mid) < SPAN else 0.5 * JIT))
            if turn % 2:
                rank = [-x for x in rank]
            else:
                late = run([rank[i] + cost[i] for i in range(n)], after, before, True)
                rank = [late[i] + cost[i] for i in range(n)]
        _plans[key] = best
    best = _plans[key]
    for i in range(n):
        ops[i]["start"], ops[i]["end"] = best[1][i], best[0]
    return sorted(range(n), key=lambda i: (best[1][i], i))


def emit(g, T, ops, order):
    queue = {"v": g.vector, "a": g.scalar, "p": g.tensor, "g": g, "s": g.sync}
    count, seen = {}, {}
    for at, i in enumerate(order):
        o = ops[i]
        q = o["q"]
        sem = o["sem"] or "e" + q
        if q != "n":
            know = seen.setdefault(q, {})
            for j in sorted(o["dep"], key=lambda k: -ops[k]["at"]):
                s, c = ops[j]["mark"]
                if know.get(s, 0) < c and not (q == "p" and ops[j]["q"] == "p"):
                    queue[q].wait_ge(T.sem[s], c)
                    know[s] = c
                    for s2, c2 in ops[j]["know"].items():
                        know[s2] = max(know.get(s2, 0), c2)
            ins = o["call"](queue[q])
            if not o.get("remote"):
                ins.then_inc(T.sem[sem], o["inc"])
        count[sem] = count.get(sem, 0) + o["inc"]
        o["mark"], o["at"], o["know"] = (sem, count[sem]), at, dict(seen.get(q, {}))
    for s in sorted(count):
        g.wait_ge(T.sem[s], count[s])


def rank_program(g, core, T, topo):
    rank = T.rank_of(core)
    if rank is not None:
        ops = build(T, topo, core, rank)
        emit(g, T, ops, plan(ops))
        return
    for r, src in enumerate(T.cores):
        for t in range(R):
            dst = T.cores[r ^ STEP[t]]
            if relay(T, topo, src, dst) == core:
                rid, pid = topo.addr(dst, core)
                mask = topo.mask(core, dst)
                g.wait_ge(T.sem.hop, 2 * len(topo.engines(src, core)))
                g.remote_dma(T["lc%d" % t][:].bitcast(dt.uint8), T.hq[:].bitcast(dt.uint8), T.sem["arr%d" % t], T.sem.hopo, pid, rid, mask)
                g.remote_dma(T["ls%d" % t][:], T.hs[:], T.sem["arr%d" % t], T.sem.hopo, pid, rid, mask)
                g.wait_ge(T.sem.hopo, 2 * len(topo.engines(core, dst)))
